import numpy as np
import ml_dtypes


def mxq(x, axis, fmt="e4m3"):
    dtype, down = {"e4m3": (ml_dtypes.float8_e4m3fn, 7), "e5m2": (ml_dtypes.float8_e5m2, 14)}[fmt]
    v = np.moveaxis(np.asarray(x, np.float32).astype(ml_dtypes.bfloat16).astype(np.float64), axis, -1)
    blocks = v.reshape(v.shape[:-1] + (-1, 32))
    amax = np.abs(blocks).max(-1, keepdims=True)
    byte = np.maximum(np.where(amax > 0, np.frexp(amax)[1] - 1 + 127, 0) - down, 1)
    scale = np.exp2(byte - 127.0)
    codes = (blocks / scale).astype(np.float32).astype(dtype).astype(np.float64)
    return np.moveaxis((codes * scale).reshape(v.shape), -1, axis)


WIDE = False


def mx_kscale(k):
    if not WIDE:
        return np.ones(k)
    levels = np.array([10, -10, 5, -5, 0])
    if k % 512:
        return np.exp2(np.random.permutation(np.resize(levels, k // 32))).repeat(32)
    a = np.empty((k // 512, 16))
    for p in range(k // 512):
        a[p, :8] = np.random.permutation(np.resize(levels, 8))
        for g in range(8):
            far = levels[np.abs(levels - a[p, g]) >= 10]
            a[p, g + 8] = far[np.random.randint(len(far))]
    return np.exp2(a.ravel()).repeat(32)


def f64(x):
    return np.asarray(x).astype(np.float64)


def striped(idx):
    return np.tile(idx.reshape(-1, 16).T, (8, 1)).astype(np.uint16)


def unstriped(offs):
    return offs[:16].T.reshape(-1).astype(np.int64)


E2M1 = np.array([0.0, 0.5, 1.0, 1.5, 2.0, 3.0, 4.0, 6.0, -0.0, -0.5, -1.0, -1.5, -2.0, -3.0, -4.0, -6.0])


def pack_weight(w, fmt):
    k, n = w.shape
    w = f64(np.asarray(w, np.float32).astype(ml_dtypes.bfloat16)).reshape(k // 32, 32, n)
    amax = np.abs(w).max(1)
    if fmt == "e4m3":
        byte = np.frexp(amax)[1] - 1 + 127 - 7
    else:
        mant, ex = np.frexp(amax / 6.0)
        byte = np.where(mant > 0.5, ex, ex - 1) + 127
    byte = np.clip(np.where(amax > 0, byte, 1), 1, 254)
    scaled = (w * np.exp2(127.0 - byte)[:, None, :]).reshape(k, n).astype(np.float32)
    by_word = np.ascontiguousarray(scaled.reshape(k // 512, 128, 4, n).transpose(0, 1, 3, 2))
    if fmt == "e4m3":
        words = by_word.astype(ml_dtypes.float8_e4m3fn).view(np.uint8)
    else:
        c = by_word.astype(ml_dtypes.float4_e2m1fn).view(np.uint8) & 0xF
        words = (c[..., 0::2] | (c[..., 1::2] << 4)).reshape(k // 512, 128, 2 * n)
    return np.ascontiguousarray(words), np.ascontiguousarray(byte.astype(np.uint8).reshape(k // 512, 16, n))


def unpack_weight(words, scales, fmt):
    g, _, n = scales.shape
    words = np.ascontiguousarray(words).reshape(g, 128, n, -1)
    if fmt == "e4m3":
        vals = words.view(ml_dtypes.float8_e4m3fn).astype(np.float64)
    else:
        nib = np.empty((g, 128, n, 4), np.uint8)
        nib[..., 0::2] = words & 0xF
        nib[..., 1::2] = words >> 4
        vals = E2M1[nib]
    vals = vals * np.repeat(np.exp2(scales.astype(np.float64) - 127.0), 8, axis=1)[..., None]
    return vals.transpose(0, 1, 3, 2).reshape(g * 512, n)


def relu(v):
    return np.maximum(v, 0.0)


K, T, E, C, N = 1536, 512, 8, 128, 512
M = 384


def by_expert(wq, xq):
    return np.concatenate([wq[e].T @ xq[:, e * C:(e + 1) * C] for e in range(E)], axis=1)


def setup_inputs():
    n = np.random.standard_normal
    s = mx_kscale(K)[:, None]
    v = mx_kscale(N)
    first = np.random.permutation(np.repeat(np.arange(E), T // E))
    second = (first + 1 + np.random.permutation(np.repeat(np.arange(E - 1), -(-T // (E - 1)))[:T])) % E
    while np.bincount(second, minlength=E).max() != T // E:
        load = np.bincount(second, minlength=E); hi, lo = int(load.argmax()), int(load.argmin())
        t = np.flatnonzero((second == hi) & (first != lo))[0]; second[t] = lo
    slot_token = np.empty(E * C, np.int64); pos = np.empty((2, T), np.int64); fill = np.zeros(E, np.int64)
    place = np.stack([np.random.permutation(C) for _ in range(E)])
    for r, deal in enumerate((first, second)):
        for t in np.random.permutation(T):
            e = deal[t]; j = e * C + place[e, fill[e]]; fill[e] += 1; slot_token[j] = t; pos[r, t] = j
    g = np.random.uniform(0.2, 0.8, T)
    w = [pack_weight(m, "e2m1") for m in n((E, K, N)) / np.sqrt(K) / s[None] * v[None, None, :]]
    return {
        "xT": (n((K, T)) * s).astype(np.float32),
        "w_words": np.stack([m[0] for m in w]),
        "w_scales": np.stack([m[1] for m in w]),
        "b": (0.3 * n((N, E)) * v[:, None]).astype(np.float32),
        "wp": (n((N, M)) / np.sqrt(N) / v[:, None]).astype(np.float32),
        "gate": np.stack([np.tile(g, (N, 1)), np.tile(1.0 - g, (N, 1))]).astype(np.float32),
        "offs": striped(slot_token),
        "pos1": striped(pos[0]),
        "pos2": striped(pos[1]),
    }


def reference(xT, w_words, w_scales, b, wp, gate, offs, pos1, pos2):
    idx = unstriped(offs)
    w = np.stack([unpack_weight(w_words[e], w_scales[e], "e2m1") for e in range(E)])
    xq = mxq(f64(xT)[:, idx], 0, "e4m3")
    y = by_expert(w, xq)
    y = relu(y + np.repeat(f64(b), C, axis=1))
    c = f64(gate[0]) * y[:, unstriped(pos1)] + f64(gate[1]) * y[:, unstriped(pos2)]
    return mxq(f64(wp), 0, "e4m3").T @ mxq(c, 0, "e4m3")

@@ -1,0 +1,196 @@
+from contextlib import ExitStack
+
+import concourse.mybir as mybir
+from concourse.masks import make_identity
+
+K, T, E, C, N, M = 1536, 512, 8, 128, 512, 384
+P = 128
+A = 3
+R = 4
+HALF = 256
+WINDOW = 1376
+FLOPS = 2 * K * N * E * C + 2 * N * M * T
+BYTES = 4 * K * T + E * K * N // 2 + E * K * N // 32 + 4 * N * E + 4 * N * M + 4 * 2 * T + 2 * 128 * 128 + 4 * M * T
+
+F32 = mybir.dt.float32
+BF16 = mybir.dt.bfloat16
+I32 = mybir.dt.int32
+U32 = mybir.dt.uint32
+U16 = mybir.dt.uint16
+U8 = mybir.dt.uint8
+FP8X4 = mybir.dt.float8_e4m3fn_x4
+FP4X4 = mybir.dt.float4_e2m1fn_x4
+ACT = mybir.ActivationFunctionType
+ALU = mybir.AluOpType
+
+
+def tile_moe_nxt_lin_relu_kernel(tc, xT, w_words, w_scales, b, wp, gate, offs, pos1, pos2, out):
+    nc = tc.nc
+    with ExitStack() as ctx:
+        keep = ctx.enter_context(tc.tile_pool(name="keep", bufs=1))
+        late = ctx.enter_context(tc.tile_pool(name="late", bufs=1))
+        ring = ctx.enter_context(tc.tile_pool(name="ring", bufs=3))
+        acc_pool = ctx.enter_context(tc.psum_pool(name="acc_pool", bufs=4))
+        turn_pool = ctx.enter_context(tc.psum_pool(name="turn_pool", bufs=4))
+
+        offs_t = keep.tile([P, E * C // 16], U16, name="offs_t")
+        pos1_t = keep.tile([P, T // 16], U16, name="pos1_t")
+        pos2_t = keep.tile([P, T // 16], U16, name="pos2_t")
+        x_raw = [keep.tile([P, 4, T], F32, name=f"x_raw{a}") for a in range(A)]
+        w_t = [keep.tile([P, 2 * A, 2 * N], U8, name=f"w_t{i}", align_bytes=64) for i in range(E // 2)]
+        ws_t = keep.tile([P, E * A, N], U8, name="ws_t", align_bytes=64)
+        b_t = keep.tile([P, R, E], F32, name="b_t")
+
+        nc.vector.memset(ws_t[:].rearrange("p g n -> p (g n)").bitcast(I32), 0)
+
+        nc.sync.dma_start(offs_t[:], offs)
+        for a in range(A):
+            nc.sync.dma_start(out=x_raw[a][:], in_=xT[512 * a : 512 * (a + 1), :].rearrange("(p j) t -> p j t", j=4))
+        nc.sync.dma_start(out=b_t[:], in_=b.rearrange("(p r) e -> p r e", r=R))
+        scale_rows = w_scales.rearrange("e a q n -> q (e a) n")
+        for i in range(4):
+            nc.sync.dma_start(out=ws_t[i:P:32, :, :].bitcast(I32), in_=scale_rows[i:16:4, :, :].bitcast(I32))
+        for i in range(E // 2):
+            nc.sync.dma_start(out=w_t[i][:].bitcast(I32), in_=w_words[2 * i : 2 * i + 2].rearrange("e a p c -> p (e a) c").bitcast(I32))
+
+        nc.sync.dma_start(pos1_t[:], pos1)
+        nc.sync.dma_start(pos2_t[:], pos2)
+        gate_t = keep.tile([P, 2, T], F32, name="gate_t")
+        nc.sync.dma_start(out=gate_t[:], in_=gate[:, 0:P, :].rearrange("g p t -> p g t"))
+        wp_raw = keep.tile([P, 4, M], F32, name="wp_raw")
+        nc.sync.dma_start(out=wp_raw[:], in_=wp.rearrange("(p j) f -> p j f", j=4))
+
+        ident = keep.tile([P, P], F32, name="ident")
+        make_identity(nc, ident[:])
+
+        codes = [keep.tile([P, WINDOW], I32, name=f"codes{a}", align_bytes=64) for a in range(A)]
+        for a in range(A):
+            nc.vector.memset(codes[a][:, T:WINDOW], 0)
+        planes = late.tile([P, WINDOW], U8, name="planes", tag="late", align_bytes=64)
+        packed = keep.tile([P, E * C], U8, name="packed", align_bytes=64)
+        slot_planes = [packed] + [keep.tile([P, E * C], U8, name=f"slot_planes{a}", align_bytes=64) for a in range(1, A)]
+        nc.gpsimd.memset(planes[:].bitcast(I32), 0)
+        for a in range(1, A):
+            nc.gpsimd.memset(slot_planes[a][:].bitcast(I32), 0)
+
+        def quantise_pass(a):
+            x_b = keep.tile([P, T, 4], BF16, name=f"x_b{a}", align_bytes=64)
+            for h in range(2):
+                dst = x_b[:, h * HALF : (h + 1) * HALF, :].rearrange("p (c i) j -> p c j i", i=4)
+                src = x_raw[a][:, :, h * HALF : (h + 1) * HALF].rearrange("p j (c i) -> p c j i", i=4)
+                if a == 0 or h == 1:
+                    nc.vector.tensor_copy(out=dst, in_=src)
+                else:
+                    nc.scalar.activation(out=dst, in_=src, func=ACT.Copy)
+            nc.vector.quantize_mx(
+                out=codes[a][:, 0:T].bitcast(FP8X4), scales=planes[4 * a : P, 0:T], in_=x_b[:].rearrange("p c j -> p (c j)")
+            )
+
+        def gather(slots, window, e0, e1):
+            nc.vector.tensor_copy(out=slots[:, e0 * C : e1 * C], in_=window.indirect(offs_t[:, e0 * C // 16 : e1 * C // 16]))
+
+        y = [keep.tile([P, E * C], F32, name=f"y{r}") for r in range(R)]
+
+        def multiply(e):
+            slots = slice(e * C, (e + 1) * C)
+            acc = acc_pool.tile([P, N], F32)
+            for a in range(A):
+                nc.tensor.matmul_mx(
+                    out=acc[:],
+                    lhsT=slot_codes[a][:, slots].bitcast(FP8X4),
+                    lhsT_scale=slot_planes[a][:, slots],
+                    rhs=w_t[e // 2][:, e % 2 * A + a, :].bitcast(FP4X4),
+                    rhs_scale=ws_t[:, e * A + a, :],
+                    start=(a == 0),
+                    stop=(a == A - 1),
+                )
+            return acc
+
+        def add_bias(e, acc):
+            z = ring.tile([P, R, P], F32)
+            nc.vector.tensor_tensor(z[:], acc[:].rearrange("s (m r) -> s r m", r=R), bias[e][:], ALU.add)
+            return z
+
+        slot_codes0 = keep.tile([P, E * C], U32, name="slot_codes0", align_bytes=64)
+        quantise_pass(0)
+        gather(slot_codes0[:], codes[0][:].bitcast(U32), 0, E)
+        quantise_pass(1)
+        quantise_pass(2)
+        gather(packed[:], planes[:], 0, E)
+        for a in range(1, A):
+            for p0, p1 in ((0, 64), (64, 100)):
+                nc.scalar.dma_start(out=slot_planes[a][p0:p1, :].bitcast(I32), in_=packed[p0 + 4 * a : p1 + 4 * a, :].bitcast(I32))
+        slot_codes12 = late.tile([P, 2, E * C], U32, name="slot_codes12", tag="late", align_bytes=64)
+        slot_codes = [slot_codes0[:], slot_codes12[:, 0, :], slot_codes12[:, 1, :]]
+        for e0 in (0, 4):
+            for a in range(1, A):
+                gather(slot_codes[a], codes[a][:].bitcast(U32), e0, e0 + 4)
+        bias = [keep.tile([P, R, P], F32, name=f"bias{e}") for e in range(E)]
+        for e in range(E):
+            spread = turn_pool.tile([P, R, P], F32, name="spread", tag="turned")
+            for r in range(R):
+                nc.tensor.transpose(spread[:, r, :], b_t[:, r, e : e + 1].to_broadcast([P, P]), ident[:])
+            nc.scalar.activation(out=bias[e][:], in_=spread[:], func=ACT.Copy)
+
+        for g in range(2):
+            turned = [turn_pool.tile([P, 4, C], F32, name=f"turned{r}", tag="turned") for r in range(R)]
+            for e in range(4 * g, 4 * g + 4):
+                z = add_bias(e, multiply(e))
+                for r in range(R):
+                    nc.tensor.transpose(turned[r][:, e % 4, :], z[:, r, :], ident[:])
+            for r in range(R):
+                nc.scalar.activation(out=y[r][:, g * 4 * C : (g + 1) * 4 * C], in_=turned[r][:].rearrange("p e s -> p (e s)"), func=ACT.Relu)
+
+        wp_b = keep.tile([P, M, 4], BF16, name="wp_b", align_bytes=64)
+        nc.scalar.activation(
+            out=wp_b[:].rearrange("p (c i) j -> p c j i", i=4), in_=wp_raw[:].rearrange("p j (c i) -> p c j i", i=4), func=ACT.Copy
+        )
+        wp_codes = keep.tile([P, M], U32, name="wp_codes", align_bytes=64)
+        wp_planes = keep.tile([P, M], U8, name="wp_planes", align_bytes=64)
+        for lo, hi in ((0, 256), (256, 384)):
+            nc.vector.quantize_mx(
+                out=wp_codes[:, lo:hi].bitcast(FP8X4), scales=wp_planes[:, lo:hi], in_=wp_b[:, lo:hi, :].rearrange("p c j -> p (c j)")
+            )
+
+        out_rows = out.rearrange("(f p) t -> p f t", p=P)
+        g1 = keep.tile([P, R, T], F32, name="g1")
+        g2 = keep.tile([P, R, T], F32, name="g2")
+
+        def fetch(r, t0, t1):
+            for g, pos_t, k in ((g1, pos1_t, 0), (g2, pos2_t, 1)):
+                nc.vector.tensor_tensor(g[:, r, t0:t1], y[r][:].indirect(pos_t[:, t0 // 16 : t1 // 16]), gate_t[:, k, t0:t1], ALU.mult)
+
+        for r in range(R - 1):
+            fetch(r, 0, T)
+        for h in range(2):
+            toks = slice(h * HALF, (h + 1) * HALF)
+            fetch(R - 1, h * HALF, (h + 1) * HALF)
+            c_b = keep.tile([P, HALF, R], BF16, name=f"c_b{h}", align_bytes=64)
+            nc.vector.tensor_tensor(
+                c_b[:].rearrange("p (c i) r -> p c r i", i=4),
+                g1[:, :, toks].rearrange("p r (c i) -> p c r i", i=4),
+                g2[:, :, toks].rearrange("p r (c i) -> p c r i", i=4),
+                ALU.add,
+            )
+            c_codes = keep.tile([P, HALF], U32, name=f"c_codes{h}", align_bytes=64)
+            c_planes = keep.tile([P, HALF], U8, name=f"c_planes{h}", align_bytes=64)
+            nc.vector.quantize_mx(out=c_codes[:].bitcast(FP8X4), scales=c_planes[:], in_=c_b[:].rearrange("p c r -> p (c r)"))
+            result = keep.tile([P, 3, HALF], F32, name=f"result{h}")
+            for f0, f1 in ((0, 2), (2, 3)):
+                acc = acc_pool.tile([P, N], F32)
+                for f in range(f0, f1):
+                    nc.tensor.matmul_mx(
+                        out=acc[:, (f - f0) * HALF : (f - f0 + 1) * HALF],
+                        lhsT=wp_codes[:, f * P : (f + 1) * P].bitcast(FP8X4),
+                        lhsT_scale=wp_planes[:, f * P : (f + 1) * P],
+                        rhs=c_codes[:].bitcast(FP8X4),
+                        rhs_scale=c_planes[:],
+                        start=True,
+                        stop=True,
+                    )
+                sums = acc[:, 0 : (f1 - f0) * HALF].rearrange("p (f t) -> p f t", t=HALF)
+                if h == 1 and f0 == 2:
+                    nc.vector.tensor_copy(out=result[:, f0:f1, :], in_=sums)
+                else:
+                    nc.scalar.activation(out=result[:, f0:f1, :], in_=sums, func=ACT.Copy)
+                nc.sync.dma_start(out=out_rows[:, f0:f1, toks], in_=result[:, f0:f1, :])

@@ -7,8 +7,12 @@ K, T, E, C, N, M = 1536, 512, 8, 128, 512, 384
 P = 128
 A = 3
 R = 4
-HALF = 256
-WINDOW = 1376
+B = T // P
+S = E * C
+WIDE = 1376
+NARROW = 704
+VECTOR_SHARE = (352, 0, 384)
+WARM = 5
 FLOPS = 2 * K * N * E * C + 2 * N * M * T
 BYTES = 4 * K * T + E * K * N // 2 + E * K * N // 32 + 4 * N * E + 4 * N * M + 4 * 2 * T + 2 * 128 * 128 + 4 * M * T
 
@@ -29,168 +33,192 @@ def tile_moe_nxt_lin_relu_kernel(tc, xT, w_words, w_scales, b, wp, gate, offs, p
     with ExitStack() as ctx:
         keep = ctx.enter_context(tc.tile_pool(name="keep", bufs=1))
         late = ctx.enter_context(tc.tile_pool(name="late", bufs=1))
-        ring = ctx.enter_context(tc.tile_pool(name="ring", bufs=3))
         acc_pool = ctx.enter_context(tc.psum_pool(name="acc_pool", bufs=4))
-        turn_pool = ctx.enter_context(tc.psum_pool(name="turn_pool", bufs=4))
+        turn_pool = ctx.enter_context(tc.psum_pool(name="turn_pool", bufs=2))
+        back_pool = ctx.enter_context(tc.psum_pool(name="back_pool", bufs=2))
 
-        offs_t = keep.tile([P, E * C // 16], U16, name="offs_t")
-        pos1_t = keep.tile([P, T // 16], U16, name="pos1_t")
-        pos2_t = keep.tile([P, T // 16], U16, name="pos2_t")
+        offs_t = keep.tile([P, S // 16], U16, name="offs_t")
+        pos_t = [keep.tile([P, T // 16], U16, name=f"pos_t{k}") for k in range(2)]
         x_raw = [keep.tile([P, 4, T], F32, name=f"x_raw{a}") for a in range(A)]
         w_t = [keep.tile([P, 2 * A, 2 * N], U8, name=f"w_t{i}", align_bytes=64) for i in range(E // 2)]
         ws_t = keep.tile([P, E * A, N], U8, name="ws_t", align_bytes=64)
         b_t = keep.tile([P, R, E], F32, name="b_t")
+        gate_in = keep.tile([P, 2, 4], F32, name="gate_in")
+        wp_raw = keep.tile([P, 4, M], F32, name="wp_raw")
 
         nc.vector.memset(ws_t[:].rearrange("p g n -> p (g n)").bitcast(I32), 0)
 
         nc.sync.dma_start(offs_t[:], offs)
         for a in range(A):
             nc.sync.dma_start(out=x_raw[a][:], in_=xT[512 * a : 512 * (a + 1), :].rearrange("(p j) t -> p j t", j=4))
-        nc.sync.dma_start(out=b_t[:], in_=b.rearrange("(p r) e -> p r e", r=R))
+        nc.sync.dma_start(out=gate_in[:], in_=gate[:, 0, :].rearrange("k (p i) -> p k i", i=4))
+        nc.sync.dma_start(out=b_t[:], in_=b.rearrange("(r p) e -> p r e", p=P))
         scale_rows = w_scales.rearrange("e a q n -> q (e a) n")
         for i in range(4):
             nc.sync.dma_start(out=ws_t[i:P:32, :, :].bitcast(I32), in_=scale_rows[i:16:4, :, :].bitcast(I32))
         for i in range(E // 2):
             nc.sync.dma_start(out=w_t[i][:].bitcast(I32), in_=w_words[2 * i : 2 * i + 2].rearrange("e a p c -> p (e a) c").bitcast(I32))
-
-        nc.sync.dma_start(pos1_t[:], pos1)
-        nc.sync.dma_start(pos2_t[:], pos2)
-        gate_t = keep.tile([P, 2, T], F32, name="gate_t")
-        nc.sync.dma_start(out=gate_t[:], in_=gate[:, 0:P, :].rearrange("g p t -> p g t"))
-        wp_raw = keep.tile([P, 4, M], F32, name="wp_raw")
+        nc.sync.dma_start(pos_t[0][:], pos1)
+        nc.sync.dma_start(pos_t[1][:], pos2)
         nc.sync.dma_start(out=wp_raw[:], in_=wp.rearrange("(p j) f -> p j f", j=4))
 
         ident = keep.tile([P, P], F32, name="ident")
         make_identity(nc, ident[:])
 
-        codes = [keep.tile([P, WINDOW], I32, name=f"codes{a}", align_bytes=64) for a in range(A)]
-        for a in range(A):
-            nc.vector.memset(codes[a][:, T:WINDOW], 0)
-        planes = late.tile([P, WINDOW], U8, name="planes", tag="late", align_bytes=64)
-        packed = keep.tile([P, E * C], U8, name="packed", align_bytes=64)
-        slot_planes = [packed] + [keep.tile([P, E * C], U8, name=f"slot_planes{a}", align_bytes=64) for a in range(1, A)]
+        codes = keep.tile([P, (A - 1) * T + WIDE], I32, name="codes", align_bytes=64)
+        nc.vector.memset(codes[:, A * T :], 0)
+        first = [(A - 1 - a) * T for a in range(A)]
+        planes = late.tile([P, WIDE], U8, name="planes", tag="late", align_bytes=64)
+        packed = keep.tile([P, S], U8, name="packed", align_bytes=64)
+        slot_planes = [packed] + [keep.tile([P, S], U8, name=f"slot_planes{a}", align_bytes=64) for a in range(1, A)]
         nc.gpsimd.memset(planes[:].bitcast(I32), 0)
         for a in range(1, A):
             nc.gpsimd.memset(slot_planes[a][:].bitcast(I32), 0)
 
         def quantise_pass(a):
             x_b = keep.tile([P, T, 4], BF16, name=f"x_b{a}", align_bytes=64)
-            for h in range(2):
-                dst = x_b[:, h * HALF : (h + 1) * HALF, :].rearrange("p (c i) j -> p c j i", i=4)
-                src = x_raw[a][:, :, h * HALF : (h + 1) * HALF].rearrange("p j (c i) -> p c j i", i=4)
-                if a == 0 or h == 1:
-                    nc.vector.tensor_copy(out=dst, in_=src)
-                else:
+            cut = T - VECTOR_SHARE[a]
+            for t0, t1 in ((0, cut), (cut, T))[: 1 if cut == T else 2]:
+                dst = x_b[:, t0:t1, :].rearrange("p (c i) j -> p c j i", i=4)
+                src = x_raw[a][:, :, t0:t1].rearrange("p j (c i) -> p c j i", i=4)
+                if t0 == 0:
                     nc.scalar.activation(out=dst, in_=src, func=ACT.Copy)
+                else:
+                    nc.vector.tensor_copy(out=dst, in_=src)
             nc.vector.quantize_mx(
-                out=codes[a][:, 0:T].bitcast(FP8X4), scales=planes[4 * a : P, 0:T], in_=x_b[:].rearrange("p c j -> p (c j)")
+                out=codes[:, first[a] : first[a] + T].bitcast(FP8X4),
+                scales=planes[4 * a : P, 0:T],
+                in_=x_b[:].rearrange("p c j -> p (c j)"),
             )
 
         def gather(slots, window, e0, e1):
             nc.vector.tensor_copy(out=slots[:, e0 * C : e1 * C], in_=window.indirect(offs_t[:, e0 * C // 16 : e1 * C // 16]))
 
-        y = [keep.tile([P, E * C], F32, name=f"y{r}") for r in range(R)]
-
-        def multiply(e):
-            slots = slice(e * C, (e + 1) * C)
-            acc = acc_pool.tile([P, N], F32)
-            for a in range(A):
-                nc.tensor.matmul_mx(
-                    out=acc[:],
-                    lhsT=slot_codes[a][:, slots].bitcast(FP8X4),
-                    lhsT_scale=slot_planes[a][:, slots],
-                    rhs=w_t[e // 2][:, e % 2 * A + a, :].bitcast(FP4X4),
-                    rhs_scale=ws_t[:, e * A + a, :],
-                    start=(a == 0),
-                    stop=(a == A - 1),
-                )
-            return acc
-
-        def add_bias(e, acc):
-            z = ring.tile([P, R, P], F32)
-            nc.vector.tensor_tensor(z[:], acc[:].rearrange("s (m r) -> s r m", r=R), bias[e][:], ALU.add)
-            return z
-
-        slot_codes0 = keep.tile([P, E * C], U32, name="slot_codes0", align_bytes=64)
+        slot_codes0 = keep.tile([P, S], U32, name="slot_codes0", align_bytes=64)
         quantise_pass(0)
-        gather(slot_codes0[:], codes[0][:].bitcast(U32), 0, E)
+        gather(slot_codes0[:], codes[:, first[0] : first[0] + WIDE].bitcast(U32), 0, E)
         quantise_pass(1)
         quantise_pass(2)
         gather(packed[:], planes[:], 0, E)
         for a in range(1, A):
-            for p0, p1 in ((0, 64), (64, 100)):
-                nc.scalar.dma_start(out=slot_planes[a][p0:p1, :].bitcast(I32), in_=packed[p0 + 4 * a : p1 + 4 * a, :].bitcast(I32))
-        slot_codes12 = late.tile([P, 2, E * C], U32, name="slot_codes12", tag="late", align_bytes=64)
+            nc.scalar.dma_start(out=slot_planes[a][0:112, :].bitcast(I32), in_=packed[4 * a : 112 + 4 * a, :].bitcast(I32))
+        slot_codes12 = late.tile([P, 2, S], U32, name="slot_codes12", tag="late", align_bytes=64)
         slot_codes = [slot_codes0[:], slot_codes12[:, 0, :], slot_codes12[:, 1, :]]
         for e0 in (0, 4):
             for a in range(1, A):
-                gather(slot_codes[a], codes[a][:].bitcast(U32), e0, e0 + 4)
-        bias = [keep.tile([P, R, P], F32, name=f"bias{e}") for e in range(E)]
-        for e in range(E):
-            spread = turn_pool.tile([P, R, P], F32, name="spread", tag="turned")
-            for r in range(R):
-                nc.tensor.transpose(spread[:, r, :], b_t[:, r, e : e + 1].to_broadcast([P, P]), ident[:])
-            nc.scalar.activation(out=bias[e][:], in_=spread[:], func=ACT.Copy)
+                gather(slot_codes[a], codes[:, first[a] : first[a] + NARROW].bitcast(U32), e0, e0 + 4)
 
-        for g in range(2):
-            turned = [turn_pool.tile([P, 4, C], F32, name=f"turned{r}", tag="turned") for r in range(R)]
-            for e in range(4 * g, 4 * g + 4):
-                z = add_bias(e, multiply(e))
-                for r in range(R):
-                    nc.tensor.transpose(turned[r][:, e % 4, :], z[:, r, :], ident[:])
-            for r in range(R):
-                nc.scalar.activation(out=y[r][:, g * 4 * C : (g + 1) * 4 * C], in_=turned[r][:].rearrange("p e s -> p (e s)"), func=ACT.Relu)
+        gate_t = keep.tile([P, 2, T], F32, name="gate_t")
+        for k in range(2):
+            spread = turn_pool.tile([P, 4, P], F32, name="spread", tag="turned")
+            for i in range(4):
+                nc.tensor.transpose(spread[:, i, :], gate_in[:, k, i : i + 1].to_broadcast([P, P]), ident[:])
+            nc.scalar.copy(out=gate_t[:, k, :].rearrange("m (p i) -> m p i", i=4), in_=spread[:].rearrange("m i p -> m p i"))
+
+        idle = back_pool.tile([P, N], F32, name="idle", tag="back")
+        for i in range(WARM):
+            nc.tensor.matmul_mx(
+                out=idle[:],
+                lhsT=w_t[0][:, 0, 0 : 2 * P].bitcast(FP4X4),
+                lhsT_scale=ws_t[:, 0, 0:P],
+                rhs=slot_codes0[:, 0:N].bitcast(FP8X4),
+                rhs_scale=packed[:, 0:N],
+                start=True,
+                stop=True,
+            )
+
+        y = [keep.tile([P, S], F32, name=f"y{r}") for r in range(R)]
+
+        def experts(e0, e1, r):
+            acc = acc_pool.tile([P, 4, C], F32, name="acc", tag="acc")
+            for e in range(e0, e1):
+                slots = slice(e * C, (e + 1) * C)
+                for a in range(A):
+                    nc.tensor.matmul_mx(
+                        out=acc[:, e - e0, :],
+                        lhsT=w_t[e // 2][:, e % 2 * A + a, 2 * P * r : 2 * P * (r + 1)].bitcast(FP4X4),
+                        lhsT_scale=ws_t[:, e * A + a, P * r : P * (r + 1)],
+                        rhs=slot_codes[a][:, slots].bitcast(FP8X4),
+                        rhs_scale=slot_planes[a][:, slots],
+                        start=(a == 0),
+                        stop=(a == A - 1),
+                    )
+            for e in range(e0, e1):
+                dst = y[r][:, e * C : (e + 1) * C]
+                if e0 == 6:
+                    nc.vector.tensor_scalar(dst, acc[:, e - e0, :], b_t[:, r, e : e + 1], 0.0, ALU.add, ALU.max)
+                else:
+                    nc.scalar.activation(out=dst, in_=acc[:, e - e0, :], func=ACT.Relu, bias=b_t[:, r, e : e + 1])
+
+        for e0, e1, r in ((0, 4, 0), (0, 4, 1), (4, 6, 0), (6, 8, 0), (4, 8, 1), (0, 4, 2), (4, 8, 2), (0, 4, 3), (4, 8, 3)):
+            experts(e0, e1, r)
+
+        gated = [[keep.tile([P, T], F32, name=f"gated{r}_{k}") for k in range(2)] for r in range(R)]
+        c_rows = [keep.tile([P, N], BF16, name=f"c_rows{t}") for t in range(B)]
+
+        def fetch(r, t0, t1):
+            for k in range(2):
+                nc.vector.tensor_tensor(gated[r][k][:, t0:t1], y[r][:].indirect(pos_t[k][:, t0 // 16 : t1 // 16]), gate_t[:, k, t0:t1], ALU.mult)
+
+        def turn(dst, r, t):
+            for k in range(2):
+                nc.tensor.matmul(dst, lhsT=gated[r][k][:, t * P : (t + 1) * P], rhs=ident[:], is_transpose=True, start=(k == 0), stop=(k == 1))
+
+        def round_rows(t, r0, r1, sums):
+            dst = c_rows[t][:].rearrange("t (u p e) -> t u p e", u=2, e=2)[:, :, 32 * r0 : 32 * r1, :]
+            nc.scalar.copy(out=dst, in_=sums.rearrange("t (p u e) -> t u p e", u=2, e=2))
+
+        for r in range(2):
+            fetch(r, 0, T)
+            turned = turn_pool.tile([P, B, P], F32, name="turned", tag="turned")
+            for t in range(B):
+                turn(turned[:, t, :], r, t)
+            for t in range(B):
+                round_rows(t, r, r + 1, turned[:, t, :])
 
         wp_b = keep.tile([P, M, 4], BF16, name="wp_b", align_bytes=64)
-        nc.scalar.activation(
-            out=wp_b[:].rearrange("p (c i) j -> p c j i", i=4), in_=wp_raw[:].rearrange("p j (c i) -> p c j i", i=4), func=ACT.Copy
-        )
         wp_codes = keep.tile([P, M], U32, name="wp_codes", align_bytes=64)
         wp_planes = keep.tile([P, M], U8, name="wp_planes", align_bytes=64)
         for lo, hi in ((0, 256), (256, 384)):
+            nc.scalar.activation(
+                out=wp_b[:, lo:hi, :].rearrange("p (c i) j -> p c j i", i=4),
+                in_=wp_raw[:, :, lo:hi].rearrange("p j (c i) -> p c j i", i=4),
+                func=ACT.Copy,
+            )
             nc.vector.quantize_mx(
                 out=wp_codes[:, lo:hi].bitcast(FP8X4), scales=wp_planes[:, lo:hi], in_=wp_b[:, lo:hi, :].rearrange("p c j -> p (c j)")
             )
 
         out_rows = out.rearrange("(f p) t -> p f t", p=P)
-        g1 = keep.tile([P, R, T], F32, name="g1")
-        g2 = keep.tile([P, R, T], F32, name="g2")
-
-        def fetch(r, t0, t1):
-            for g, pos_t, k in ((g1, pos1_t, 0), (g2, pos2_t, 1)):
-                nc.vector.tensor_tensor(g[:, r, t0:t1], y[r][:].indirect(pos_t[:, t0 // 16 : t1 // 16]), gate_t[:, k, t0:t1], ALU.mult)
-
-        for r in range(R - 1):
-            fetch(r, 0, T)
-        for h in range(2):
-            toks = slice(h * HALF, (h + 1) * HALF)
-            fetch(R - 1, h * HALF, (h + 1) * HALF)
-            c_b = keep.tile([P, HALF, R], BF16, name=f"c_b{h}", align_bytes=64)
-            nc.vector.tensor_tensor(
-                c_b[:].rearrange("p (c i) r -> p c r i", i=4),
-                g1[:, :, toks].rearrange("p r (c i) -> p c r i", i=4),
-                g2[:, :, toks].rearrange("p r (c i) -> p c r i", i=4),
-                ALU.add,
-            )
-            c_codes = keep.tile([P, HALF], U32, name=f"c_codes{h}", align_bytes=64)
-            c_planes = keep.tile([P, HALF], U8, name=f"c_planes{h}", align_bytes=64)
-            nc.vector.quantize_mx(out=c_codes[:].bitcast(FP8X4), scales=c_planes[:], in_=c_b[:].rearrange("p c r -> p (c r)"))
-            result = keep.tile([P, 3, HALF], F32, name=f"result{h}")
-            for f0, f1 in ((0, 2), (2, 3)):
-                acc = acc_pool.tile([P, N], F32)
-                for f in range(f0, f1):
-                    nc.tensor.matmul_mx(
-                        out=acc[:, (f - f0) * HALF : (f - f0 + 1) * HALF],
-                        lhsT=wp_codes[:, f * P : (f + 1) * P].bitcast(FP8X4),
-                        lhsT_scale=wp_planes[:, f * P : (f + 1) * P],
-                        rhs=c_codes[:].bitcast(FP8X4),
-                        rhs_scale=c_planes[:],
-                        start=True,
-                        stop=True,
-                    )
-                sums = acc[:, 0 : (f1 - f0) * HALF].rearrange("p (f t) -> p f t", t=HALF)
-                if h == 1 and f0 == 2:
-                    nc.vector.tensor_copy(out=result[:, f0:f1, :], in_=sums)
-                else:
-                    nc.scalar.activation(out=result[:, f0:f1, :], in_=sums, func=ACT.Copy)
-                nc.sync.dma_start(out=out_rows[:, f0:f1, toks], in_=result[:, f0:f1, :])
+        for t in range(B):
+            turned = turn_pool.tile([P, 2, P], F32, name="turned", tag="turned")
+            for r in range(2, R):
+                fetch(r, t * P, (t + 1) * P)
+                turn(turned[:, r - 2, :], r, t)
+            round_rows(t, 2, R, turned[:].rearrange("t r n -> t (r n)"))
+            back = back_pool.tile([P, 2, P], F32, name="back", tag="back")
+            pairs = c_rows[t][:].bitcast(F32)
+            for u in range(2):
+                nc.tensor.transpose(back[:, u, :], pairs[:, u * P : (u + 1) * P], ident[:])
+            c_b = keep.tile([P, 4 * P], BF16, name=f"c_b{t}", align_bytes=64)
+            nc.scalar.copy(out=c_b[:].bitcast(F32).rearrange("p (t u) -> p t u", u=2), in_=back[:].rearrange("p u t -> p t u"))
+            c_codes = keep.tile([P, P], U32, name=f"c_codes{t}", align_bytes=64)
+            c_planes = keep.tile([P, P], U8, name=f"c_planes{t}", align_bytes=64)
+            nc.vector.quantize_mx(out=c_codes[:].bitcast(FP8X4), scales=c_planes[:], in_=c_b[:])
+            acc = acc_pool.tile([P, 4, C], F32, name="acc", tag="acc")
+            for f in range(M // P):
+                nc.tensor.matmul_mx(
+                    out=acc[:, f, :],
+                    lhsT=wp_codes[:, f * P : (f + 1) * P].bitcast(FP8X4),
+                    lhsT_scale=wp_planes[:, f * P : (f + 1) * P],
+                    rhs=c_codes[:].bitcast(FP8X4),
+                    rhs_scale=c_planes[:],
+                    start=True,
+                    stop=True,
+                )
+            result = keep.tile([P, M // P, P], F32, name=f"result{t}")
+            if t % 2 == 0:
+                nc.scalar.copy(out=result[:], in_=acc[:, 0 : M // P, :])
+            else:
+                nc.vector.tensor_copy(out=result[:], in_=acc[:, 0 : M // P, :])
+            nc.sync.dma_start(out=out_rows[:, :, t * P : (t + 1) * P], in_=result[:])

@@ -40,7 +40,7 @@ def tile_moe_nxt_lin_relu_kernel(tc, xT, w_words, w_scales, b, wp, gate, offs, p
         offs_t = keep.tile([P, S // 16], U16, name="offs_t")
         pos_t = [keep.tile([P, T // 16], U16, name=f"pos_t{k}") for k in range(2)]
         x_raw = [keep.tile([P, 4, T], F32, name=f"x_raw{a}") for a in range(A)]
-        w_t = [keep.tile([P, 2 * A, 2 * N], U8, name=f"w_t{i}", align_bytes=64) for i in range(E // 2)]
+        w_t = [[keep.tile([P, 4 * A, N], U8, name=f"w_t{h}_{g}", align_bytes=64) for g in range(2)] for h in range(2)]
         ws_t = keep.tile([P, E * A, N], U8, name="ws_t", align_bytes=64)
         b_t = keep.tile([P, R, E], F32, name="b_t")
         gate_in = keep.tile([P, 2, 4], F32, name="gate_in")
@@ -53,13 +53,15 @@ def tile_moe_nxt_lin_relu_kernel(tc, xT, w_words, w_scales, b, wp, gate, offs, p
             nc.sync.dma_start(out=x_raw[a][:], in_=xT[512 * a : 512 * (a + 1), :].rearrange("(p j) t -> p j t", j=4))
         nc.sync.dma_start(out=gate_in[:], in_=gate[:, 0, :].rearrange("k (p i) -> p k i", i=4))
         nc.sync.dma_start(out=b_t[:], in_=b.rearrange("(r p) e -> p r e", p=P))
+        nc.sync.dma_start(pos_t[0][:], pos1)
+        nc.sync.dma_start(pos_t[1][:], pos2)
         scale_rows = w_scales.rearrange("e a q n -> q (e a) n")
         for i in range(4):
             nc.sync.dma_start(out=ws_t[i:P:32, :, :].bitcast(I32), in_=scale_rows[i:16:4, :, :].bitcast(I32))
-        for i in range(E // 2):
-            nc.sync.dma_start(out=w_t[i][:].bitcast(I32), in_=w_words[2 * i : 2 * i + 2].rearrange("e a p c -> p (e a) c").bitcast(I32))
-        nc.sync.dma_start(pos_t[0][:], pos1)
-        nc.sync.dma_start(pos_t[1][:], pos2)
+        word_rows = w_words.rearrange("e a p c -> p (e a) c")
+        for h in range(2):
+            for g in range(2):
+                nc.sync.dma_start(out=w_t[h][g][:].bitcast(I32), in_=word_rows[:, 4 * A * g : 4 * A * (g + 1), N * h : N * (h + 1)].bitcast(I32))
         nc.sync.dma_start(out=wp_raw[:], in_=wp.rearrange("(p j) f -> p j f", j=4))
 
         ident = keep.tile([P, P], F32, name="ident")
@@ -104,9 +106,8 @@ def tile_moe_nxt_lin_relu_kernel(tc, xT, w_words, w_scales, b, wp, gate, offs, p
             nc.scalar.dma_start(out=slot_planes[a][0:112, :].bitcast(I32), in_=packed[4 * a : 112 + 4 * a, :].bitcast(I32))
         slot_codes12 = late.tile([P, 2, S], U32, name="slot_codes12", tag="late", align_bytes=64)
         slot_codes = [slot_codes0[:], slot_codes12[:, 0, :], slot_codes12[:, 1, :]]
-        for e0 in (0, 4):
-            for a in range(1, A):
-                gather(slot_codes[a], codes[:, first[a] : first[a] + NARROW].bitcast(U32), e0, e0 + 4)
+        for a, e0, e1 in ((1, 0, 4), (2, 0, 4), (1, 4, 8), (2, 4, 6), (2, 6, 8)):
+            gather(slot_codes[a], codes[:, first[a] : first[a] + NARROW].bitcast(U32), e0, e1)
 
         gate_t = keep.tile([P, 2, T], F32, name="gate_t")
         for k in range(2):
@@ -119,8 +120,8 @@ def tile_moe_nxt_lin_relu_kernel(tc, xT, w_words, w_scales, b, wp, gate, offs, p
         for i in range(WARM):
             nc.tensor.matmul_mx(
                 out=idle[:],
-                lhsT=w_t[0][:, 0, 0 : 2 * P].bitcast(FP4X4),
-                lhsT_scale=ws_t[:, 0, 0:P],
+                lhsT=slot_codes0[:, 0:P].bitcast(FP8X4),
+                lhsT_scale=packed[:, 0:P],
                 rhs=slot_codes0[:, 0:N].bitcast(FP8X4),
                 rhs_scale=packed[:, 0:N],
                 start=True,
@@ -136,7 +137,7 @@ def tile_moe_nxt_lin_relu_kernel(tc, xT, w_words, w_scales, b, wp, gate, offs, p
                 for a in range(A):
                     nc.tensor.matmul_mx(
                         out=acc[:, e - e0, :],
-                        lhsT=w_t[e // 2][:, e % 2 * A + a, 2 * P * r : 2 * P * (r + 1)].bitcast(FP4X4),
+                        lhsT=w_t[r // 2][e // 4][:, e % 4 * A + a, 2 * P * (r % 2) : 2 * P * (r % 2 + 1)].bitcast(FP4X4),
                         lhsT_scale=ws_t[:, e * A + a, P * r : P * (r + 1)],
                         rhs=slot_codes[a][:, slots].bitcast(FP8X4),
                         rhs_scale=slot_planes[a][:, slots],
@@ -150,7 +151,7 @@ def tile_moe_nxt_lin_relu_kernel(tc, xT, w_words, w_scales, b, wp, gate, offs, p
                 else:
                     nc.scalar.activation(out=dst, in_=acc[:, e - e0, :], func=ACT.Relu, bias=b_t[:, r, e : e + 1])
 
-        for e0, e1, r in ((0, 4, 0), (0, 4, 1), (4, 6, 0), (6, 8, 0), (4, 8, 1), (0, 4, 2), (4, 8, 2), (0, 4, 3), (4, 8, 3)):
+        for e0, e1, r in ((0, 4, 0), (0, 4, 1), (4, 6, 0), (6, 8, 0), (4, 8, 1), (0, 4, 2), (0, 4, 3), (4, 8, 2), (4, 8, 3)):
             experts(e0, e1, r)
 
         gated = [[keep.tile([P, T], F32, name=f"gated{r}_{k}") for k in range(2)] for r in range(R)]
@@ -168,7 +169,7 @@ def tile_moe_nxt_lin_relu_kernel(tc, xT, w_words, w_scales, b, wp, gate, offs, p
             dst = c_rows[t][:].rearrange("t (u p e) -> t u p e", u=2, e=2)[:, :, 32 * r0 : 32 * r1, :]
             nc.scalar.copy(out=dst, in_=sums.rearrange("t (p u e) -> t u p e", u=2, e=2))
 
-        for r in range(2):
+        for r in range(R - 1):
             fetch(r, 0, T)
             turned = turn_pool.tile([P, B, P], F32, name="turned", tag="turned")
             for t in range(B):
@@ -191,11 +192,10 @@ def tile_moe_nxt_lin_relu_kernel(tc, xT, w_words, w_scales, b, wp, gate, offs, p
 
         out_rows = out.rearrange("(f p) t -> p f t", p=P)
         for t in range(B):
-            turned = turn_pool.tile([P, 2, P], F32, name="turned", tag="turned")
-            for r in range(2, R):
-                fetch(r, t * P, (t + 1) * P)
-                turn(turned[:, r - 2, :], r, t)
-            round_rows(t, 2, R, turned[:].rearrange("t r n -> t (r n)"))
+            turned = turn_pool.tile([P, P], F32, name="turned", tag="turned")
+            fetch(R - 1, t * P, (t + 1) * P)
+            turn(turned[:], R - 1, t)
+            round_rows(t, R - 1, R, turned[:])
             back = back_pool.tile([P, 2, P], F32, name="back", tag="back")
             pairs = c_rows[t][:].bitcast(F32)
             for u in range(2):

@@ -13,6 +13,7 @@ WIDE = 1376
 NARROW = 704
 VECTOR_SHARE = (352, 0, 384)
 WARM = 5
+GAP = 64
 FLOPS = 2 * K * N * E * C + 2 * N * M * T
 BYTES = 4 * K * T + E * K * N // 2 + E * K * N // 32 + 4 * N * E + 4 * N * M + 4 * 2 * T + 2 * 128 * 128 + 4 * M * T
 
@@ -40,28 +41,28 @@ def tile_moe_nxt_lin_relu_kernel(tc, xT, w_words, w_scales, b, wp, gate, offs, p
         offs_t = keep.tile([P, S // 16], U16, name="offs_t")
         pos_t = [keep.tile([P, T // 16], U16, name=f"pos_t{k}") for k in range(2)]
         x_raw = [keep.tile([P, 4, T], F32, name=f"x_raw{a}") for a in range(A)]
-        w_t = [[keep.tile([P, 4 * A, N], U8, name=f"w_t{h}_{g}", align_bytes=64) for g in range(2)] for h in range(2)]
-        ws_t = keep.tile([P, E * A, N], U8, name="ws_t", align_bytes=64)
+        w_t = [[keep.tile([P, 4 * A, N + GAP], U8, name=f"w_t{h}_{g}", tag=f"w{h}_{g}", align_bytes=64) for g in range(2)] for h in range(2)]
+        ws_t = keep.tile([P, E * A, N + GAP], U8, name="ws_t", align_bytes=64)
         b_t = keep.tile([P, R, E], F32, name="b_t")
-        gate_in = keep.tile([P, 2, 4], F32, name="gate_in")
+        gate_in = keep.tile([P, 2, 8], F32, name="gate_in")
         wp_raw = keep.tile([P, 4, M], F32, name="wp_raw")
 
-        nc.vector.memset(ws_t[:].rearrange("p g n -> p (g n)").bitcast(I32), 0)
+        nc.vector.memset(ws_t[:, :, 0:N].bitcast(I32), 0)
 
         nc.sync.dma_start(offs_t[:], offs)
         for a in range(A):
             nc.sync.dma_start(out=x_raw[a][:], in_=xT[512 * a : 512 * (a + 1), :].rearrange("(p j) t -> p j t", j=4))
-        nc.sync.dma_start(out=gate_in[:], in_=gate[:, 0, :].rearrange("k (p i) -> p k i", i=4))
+        nc.sync.dma_start(out=gate_in[:, :, 0:4], in_=gate[:, 0, :].rearrange("k (p i) -> p k i", i=4))
         nc.sync.dma_start(out=b_t[:], in_=b.rearrange("(r p) e -> p r e", p=P))
         nc.sync.dma_start(pos_t[0][:], pos1)
         nc.sync.dma_start(pos_t[1][:], pos2)
         scale_rows = w_scales.rearrange("e a q n -> q (e a) n")
         for i in range(4):
-            nc.sync.dma_start(out=ws_t[i:P:32, :, :].bitcast(I32), in_=scale_rows[i:16:4, :, :].bitcast(I32))
+            nc.sync.dma_start(out=ws_t[i:P:32, :, 0:N].bitcast(I32), in_=scale_rows[i:16:4, :, :].bitcast(I32))
         word_rows = w_words.rearrange("e a p c -> p (e a) c")
         for h in range(2):
             for g in range(2):
-                nc.sync.dma_start(out=w_t[h][g][:].bitcast(I32), in_=word_rows[:, 4 * A * g : 4 * A * (g + 1), N * h : N * (h + 1)].bitcast(I32))
+                nc.sync.dma_start(out=w_t[h][g][:, :, 0:N].bitcast(I32), in_=word_rows[:, 4 * A * g : 4 * A * (g + 1), N * h : N * (h + 1)].bitcast(I32))
         nc.sync.dma_start(out=wp_raw[:], in_=wp.rearrange("(p j) f -> p j f", j=4))
 
         ident = keep.tile([P, P], F32, name="ident")
@@ -177,7 +178,7 @@ def tile_moe_nxt_lin_relu_kernel(tc, xT, w_words, w_scales, b, wp, gate, offs, p
             for t in range(B):
                 round_rows(t, r, r + 1, turned[:, t, :])
 
-        wp_b = keep.tile([P, M, 4], BF16, name="wp_b", align_bytes=64)
+        wp_b = keep.tile([P, M, 4], BF16, name="wp_b", tag="w1_1", align_bytes=64)
         wp_codes = keep.tile([P, M], U32, name="wp_codes", align_bytes=64)
         wp_planes = keep.tile([P, M], U8, name="wp_planes", align_bytes=64)
         for lo, hi in ((0, 256), (256, 384)):
@@ -216,9 +217,9 @@ def tile_moe_nxt_lin_relu_kernel(tc, xT, w_words, w_scales, b, wp, gate, offs, p
                     start=True,
                     stop=True,
                 )
-            result = keep.tile([P, M // P, P], F32, name=f"result{t}")
+            result = keep.tile([P, M // P, P + GAP // 4], F32, name=f"result{t}")[:, :, 0:P]
             if t % 2 == 0:
-                nc.scalar.copy(out=result[:], in_=acc[:, 0 : M // P, :])
+                nc.scalar.copy(out=result, in_=acc[:, 0 : M // P, :])
             else:
-                nc.vector.tensor_copy(out=result[:], in_=acc[:, 0 : M // P, :])
-            nc.sync.dma_start(out=out_rows[:, :, t * P : (t + 1) * P], in_=result[:])
+                nc.vector.tensor_copy(out=result, in_=acc[:, 0 : M // P, :])
+            nc.sync.dma_start(out=out_rows[:, :, t * P : (t + 1) * P], in_=result)

@@ -41,11 +41,10 @@ def tile_moe_nxt_lin_relu_kernel(tc, xT, w_words, w_scales, b, wp, gate, offs, p
         offs_t = keep.tile([P, S // 16], U16, name="offs_t")
         pos_t = [keep.tile([P, T // 16], U16, name=f"pos_t{k}") for k in range(2)]
         x_raw = [keep.tile([P, 4, T], F32, name=f"x_raw{a}") for a in range(A)]
-        w_t = [[keep.tile([P, 4 * A, N + GAP], U8, name=f"w_t{h}_{g}", tag=f"w{h}_{g}", align_bytes=64) for g in range(2)] for h in range(2)]
+        w_first = keep.tile([P, 4 * A, N], U8, name="w_first", align_bytes=64)
         ws_t = keep.tile([P, E * A, N + GAP], U8, name="ws_t", align_bytes=64)
         b_t = keep.tile([P, R, E], F32, name="b_t")
         gate_in = keep.tile([P, 2, 8], F32, name="gate_in")
-        wp_raw = keep.tile([P, 4, M], F32, name="wp_raw")
 
         nc.vector.memset(ws_t[:, :, 0:N].bitcast(I32), 0)
 
@@ -60,18 +59,19 @@ def tile_moe_nxt_lin_relu_kernel(tc, xT, w_words, w_scales, b, wp, gate, offs, p
         for i in range(4):
             nc.sync.dma_start(out=ws_t[i:P:32, :, 0:N].bitcast(I32), in_=scale_rows[i:16:4, :, :].bitcast(I32))
         word_rows = w_words.rearrange("e a p c -> p (e a) c")
-        for h in range(2):
-            for g in range(2):
-                nc.sync.dma_start(out=w_t[h][g][:, :, 0:N].bitcast(I32), in_=word_rows[:, 4 * A * g : 4 * A * (g + 1), N * h : N * (h + 1)].bitcast(I32))
-        nc.sync.dma_start(out=wp_raw[:], in_=wp.rearrange("(p j) f -> p j f", j=4))
+
+        def load_words(dst, h, g):
+            nc.sync.dma_start(out=dst.bitcast(I32), in_=word_rows[:, 4 * A * g : 4 * A * (g + 1), N * h : N * (h + 1)].bitcast(I32))
+
+        load_words(w_first[:], 0, 0)
 
         ident = keep.tile([P, P], F32, name="ident")
         make_identity(nc, ident[:])
 
-        codes = keep.tile([P, (A - 1) * T + WIDE], I32, name="codes", align_bytes=64)
+        codes = keep.tile([P, (A - 1) * T + WIDE], I32, name="codes", tag="codes", align_bytes=64)
         nc.vector.memset(codes[:, A * T :], 0)
         first = [(A - 1 - a) * T for a in range(A)]
-        planes = late.tile([P, WIDE], U8, name="planes", tag="late", align_bytes=64)
+        planes = late.tile([P, WIDE], U8, name="planes", offset=8 * S - 64, align_bytes=64)
         packed = keep.tile([P, S], U8, name="packed", align_bytes=64)
         slot_planes = [packed] + [keep.tile([P, S], U8, name=f"slot_planes{a}", align_bytes=64) for a in range(1, A)]
         nc.gpsimd.memset(planes[:].bitcast(I32), 0)
@@ -104,11 +104,18 @@ def tile_moe_nxt_lin_relu_kernel(tc, xT, w_words, w_scales, b, wp, gate, offs, p
         quantise_pass(2)
         gather(packed[:], planes[:], 0, E)
         for a in range(1, A):
-            nc.scalar.dma_start(out=slot_planes[a][0:112, :].bitcast(I32), in_=packed[4 * a : 112 + 4 * a, :].bitcast(I32))
-        slot_codes12 = late.tile([P, 2, S], U32, name="slot_codes12", tag="late", align_bytes=64)
+            nc.sync.dma_start(out=slot_planes[a][0:112, :].bitcast(I32), in_=packed[4 * a : 112 + 4 * a, :].bitcast(I32))
+        w_rest = late.tile([P, 3, 4 * A, N], U8, name="w_rest", offset=8 * S, align_bytes=64)
+        w_t = [[w_first[:], w_rest[:, 0]], [w_rest[:, 1], w_rest[:, 2]]]
+        for h, g in ((0, 1), (1, 0), (1, 1)):
+            load_words(w_t[h][g], h, g)
+        slot_codes12 = late.tile([P, 2, S], U32, name="slot_codes12", offset=0, align_bytes=64)
         slot_codes = [slot_codes0[:], slot_codes12[:, 0, :], slot_codes12[:, 1, :]]
         for a, e0, e1 in ((1, 0, 4), (2, 0, 4), (1, 4, 8), (2, 4, 6), (2, 6, 8)):
             gather(slot_codes[a], codes[:, first[a] : first[a] + NARROW].bitcast(U32), e0, e1)
+
+        wp_raw = keep.tile([P, 4, M], F32, name="wp_raw", tag="codes", align_bytes=64)
+        nc.sync.dma_start(out=wp_raw[:], in_=wp.rearrange("(p j) f -> p j f", j=4))
 
         gate_t = keep.tile([P, 2, T], F32, name="gate_t")
         for k in range(2):
@@ -178,7 +185,7 @@ def tile_moe_nxt_lin_relu_kernel(tc, xT, w_words, w_scales, b, wp, gate, offs, p
             for t in range(B):
                 round_rows(t, r, r + 1, turned[:, t, :])
 
-        wp_b = keep.tile([P, M, 4], BF16, name="wp_b", tag="w1_1", align_bytes=64)
+        wp_b = late.tile([P, M, 4], BF16, name="wp_b", offset=0, align_bytes=64)
         wp_codes = keep.tile([P, M], U32, name="wp_codes", align_bytes=64)
         wp_planes = keep.tile([P, M], U8, name="wp_planes", align_bytes=64)
         for lo, hi in ((0, 256), (256, 384)):

@@ -52,21 +52,22 @@ def tile_moe_nxt_lin_relu_kernel(tc, xT, w_words, w_scales, b, wp, gate, offs, p
         for a in range(A):
             nc.sync.dma_start(out=x_raw[a][:], in_=xT[512 * a : 512 * (a + 1), :].rearrange("(p j) t -> p j t", j=4))
         nc.sync.dma_start(out=gate_in[:, :, 0:4], in_=gate[:, 0, :].rearrange("k (p i) -> p k i", i=4))
-        nc.sync.dma_start(out=b_t[:], in_=b.rearrange("(r p) e -> p r e", p=P))
         nc.sync.dma_start(pos_t[0][:], pos1)
         nc.sync.dma_start(pos_t[1][:], pos2)
+        word_rows = w_words.rearrange("e a p c -> p (e a) c")
+
+        def load_words(dst, h, e0, e1):
+            rows = slice(e0 % 4 * A, ((e1 - 1) % 4 + 1) * A)
+            nc.sync.dma_start(out=dst[:, rows, :].bitcast(I32), in_=word_rows[:, A * e0 : A * e1, N * h : N * (h + 1)].bitcast(I32))
+
+        load_words(w_first[:], 0, 0, 4)
         scale_rows = w_scales.rearrange("e a q n -> q (e a) n")
         for i in range(4):
             nc.sync.dma_start(out=ws_t[i:P:32, :, 0:N].bitcast(I32), in_=scale_rows[i:16:4, :, :].bitcast(I32))
-        word_rows = w_words.rearrange("e a p c -> p (e a) c")
-
-        def load_words(dst, h, g):
-            nc.sync.dma_start(out=dst.bitcast(I32), in_=word_rows[:, 4 * A * g : 4 * A * (g + 1), N * h : N * (h + 1)].bitcast(I32))
-
-        load_words(w_first[:], 0, 0)
 
         ident = keep.tile([P, P], F32, name="ident")
         make_identity(nc, ident[:])
+        nc.gpsimd.dma_start(out=b_t[:], in_=b.rearrange("(r p) e -> p r e", p=P))
 
         codes = keep.tile([P, (A - 1) * T + WIDE], I32, name="codes", tag="codes", align_bytes=64)
         nc.vector.memset(codes[:, A * T :], 0)
@@ -74,9 +75,9 @@ def tile_moe_nxt_lin_relu_kernel(tc, xT, w_words, w_scales, b, wp, gate, offs, p
         planes = late.tile([P, WIDE], U8, name="planes", offset=8 * S - 64, align_bytes=64)
         packed = keep.tile([P, S], U8, name="packed", align_bytes=64)
         slot_planes = [packed] + [keep.tile([P, S], U8, name=f"slot_planes{a}", align_bytes=64) for a in range(1, A)]
-        nc.gpsimd.memset(planes[:].bitcast(I32), 0)
+        nc.vector.memset(planes[:].bitcast(I32), 0)
         for a in range(1, A):
-            nc.gpsimd.memset(slot_planes[a][:].bitcast(I32), 0)
+            nc.vector.memset(slot_planes[a][:].bitcast(I32), 0)
 
         def quantise_pass(a):
             x_b = keep.tile([P, T, 4], BF16, name=f"x_b{a}", align_bytes=64)
@@ -107,8 +108,8 @@ def tile_moe_nxt_lin_relu_kernel(tc, xT, w_words, w_scales, b, wp, gate, offs, p
             nc.sync.dma_start(out=slot_planes[a][0:112, :].bitcast(I32), in_=packed[4 * a : 112 + 4 * a, :].bitcast(I32))
         w_rest = late.tile([P, 3, 4 * A, N], U8, name="w_rest", offset=8 * S, align_bytes=64)
         w_t = [[w_first[:], w_rest[:, 0]], [w_rest[:, 1], w_rest[:, 2]]]
-        for h, g in ((0, 1), (1, 0), (1, 1)):
-            load_words(w_t[h][g], h, g)
+        for h, e0, e1 in ((0, 4, 8), (1, 0, 4), (1, 4, 8)):
+            load_words(w_t[h][e0 // 4], h, e0, e1)
         slot_codes12 = late.tile([P, 2, S], U32, name="slot_codes12", offset=0, align_bytes=64)
         slot_codes = [slot_codes0[:], slot_codes12[:, 0, :], slot_codes12[:, 1, :]]
         for a, e0, e1 in ((1, 0, 4), (2, 0, 4), (1, 4, 8), (2, 4, 6), (2, 6, 8)):
@@ -199,6 +200,7 @@ def tile_moe_nxt_lin_relu_kernel(tc, xT, w_words, w_scales, b, wp, gate, offs, p
             )
 
         out_rows = out.rearrange("(f p) t -> p f t", p=P)
+        c_b = [keep.tile([P, 4 * P], BF16, name=f"c_b{t}", align_bytes=64) for t in range(B)]
         for t in range(B):
             turned = turn_pool.tile([P, P], F32, name="turned", tag="turned")
             fetch(R - 1, t * P, (t + 1) * P)
@@ -208,11 +210,12 @@ def tile_moe_nxt_lin_relu_kernel(tc, xT, w_words, w_scales, b, wp, gate, offs, p
             pairs = c_rows[t][:].bitcast(F32)
             for u in range(2):
                 nc.tensor.transpose(back[:, u, :], pairs[:, u * P : (u + 1) * P], ident[:])
-            c_b = keep.tile([P, 4 * P], BF16, name=f"c_b{t}", align_bytes=64)
-            nc.scalar.copy(out=c_b[:].bitcast(F32).rearrange("p (t u) -> p t u", u=2), in_=back[:].rearrange("p u t -> p t u"))
+            nc.scalar.copy(out=c_b[t][:].bitcast(F32).rearrange("p (t u) -> p t u", u=2), in_=back[:].rearrange("p u t -> p t u"))
+
+        for t in range(B):
             c_codes = keep.tile([P, P], U32, name=f"c_codes{t}", align_bytes=64)
             c_planes = keep.tile([P, P], U8, name=f"c_planes{t}", align_bytes=64)
-            nc.vector.quantize_mx(out=c_codes[:].bitcast(FP8X4), scales=c_planes[:], in_=c_b[:])
+            nc.vector.quantize_mx(out=c_codes[:].bitcast(FP8X4), scales=c_planes[:], in_=c_b[t][:])
             acc = acc_pool.tile([P, 4, C], F32, name="acc", tag="acc")
             for f in range(M // P):
                 nc.tensor.matmul_mx(

@@ -5,15 +5,19 @@ from concourse.masks import make_identity
 
 K, T, E, C, N, M = 1536, 512, 8, 128, 512, 384
 P = 128
-A = 3
-R = 4
+A = K // 512
+R = N // P
 B = T // P
 S = E * C
+G = E // 2
 WIDE = 1376
 NARROW = 704
-VECTOR_SHARE = (352, 0, 384)
-WARM = 5
+VECTOR_SHARE = (352, 160, 240)
+LIVE_ROWS = 100
 GAP = 64
+AT_W_REST = (2 * A - 1) * G * C * 4
+AT_PLANES = AT_W_REST - 64
+AT_X_FIRST = AT_W_REST + 3 * G * A * N
 FLOPS = 2 * K * N * E * C + 2 * N * M * T
 BYTES = 4 * K * T + E * K * N // 2 + E * K * N // 32 + 4 * N * E + 4 * N * M + 4 * 2 * T + 2 * 128 * 128 + 4 * M * T
 
@@ -40,27 +44,29 @@ def tile_moe_nxt_lin_relu_kernel(tc, xT, w_words, w_scales, b, wp, gate, offs, p
 
         offs_t = keep.tile([P, S // 16], U16, name="offs_t")
         pos_t = [keep.tile([P, T // 16], U16, name=f"pos_t{k}") for k in range(2)]
-        x_raw = [keep.tile([P, 4, T], F32, name=f"x_raw{a}") for a in range(A)]
-        w_first = keep.tile([P, 4 * A, N], U8, name="w_first", align_bytes=64)
+        x_raw = [late.tile([P, 4, T], F32, name="x_raw0", offset=AT_X_FIRST, align_bytes=64)]
+        x_raw = x_raw + [keep.tile([P, 4, T], F32, name=f"x_raw{a}") for a in range(1, A)]
+        w_first = keep.tile([P, G * A, N], U8, name="w_first", align_bytes=64)
         ws_t = keep.tile([P, E * A, N + GAP], U8, name="ws_t", align_bytes=64)
         b_t = keep.tile([P, R, E], F32, name="b_t")
         gate_in = keep.tile([P, 2, 8], F32, name="gate_in")
 
         nc.vector.memset(ws_t[:, :, 0:N].bitcast(I32), 0)
 
-        nc.sync.dma_start(offs_t[:], offs)
         for a in range(A):
             nc.sync.dma_start(out=x_raw[a][:], in_=xT[512 * a : 512 * (a + 1), :].rearrange("(p j) t -> p j t", j=4))
+            if a == 0:
+                nc.sync.dma_start(offs_t[:], offs)
         nc.sync.dma_start(out=gate_in[:, :, 0:4], in_=gate[:, 0, :].rearrange("k (p i) -> p k i", i=4))
         nc.sync.dma_start(pos_t[0][:], pos1)
         nc.sync.dma_start(pos_t[1][:], pos2)
+
         word_rows = w_words.rearrange("e a p c -> p (e a) c")
 
-        def load_words(dst, h, e0, e1):
-            rows = slice(e0 % 4 * A, ((e1 - 1) % 4 + 1) * A)
-            nc.sync.dma_start(out=dst[:, rows, :].bitcast(I32), in_=word_rows[:, A * e0 : A * e1, N * h : N * (h + 1)].bitcast(I32))
+        def load_words(dst, h, g):
+            nc.sync.dma_start(out=dst.bitcast(I32), in_=word_rows[:, G * A * g : G * A * (g + 1), N * h : N * (h + 1)].bitcast(I32))
 
-        load_words(w_first[:], 0, 0, 4)
+        load_words(w_first[:], 0, 0)
         scale_rows = w_scales.rearrange("e a q n -> q (e a) n")
         for i in range(4):
             nc.sync.dma_start(out=ws_t[i:P:32, :, 0:N].bitcast(I32), in_=scale_rows[i:16:4, :, :].bitcast(I32))
@@ -69,51 +75,62 @@ def tile_moe_nxt_lin_relu_kernel(tc, xT, w_words, w_scales, b, wp, gate, offs, p
         make_identity(nc, ident[:])
         nc.gpsimd.dma_start(out=b_t[:], in_=b.rearrange("(r p) e -> p r e", p=P))
 
-        codes = keep.tile([P, (A - 1) * T + WIDE], I32, name="codes", tag="codes", align_bytes=64)
+        codes = keep.tile([P, (A - 1) * T + NARROW], I32, name="codes", tag="codes", align_bytes=64)
         nc.vector.memset(codes[:, A * T :], 0)
         first = [(A - 1 - a) * T for a in range(A)]
-        planes = late.tile([P, WIDE], U8, name="planes", offset=8 * S - 64, align_bytes=64)
+        planes = late.tile([P, WIDE], U8, name="planes", offset=AT_PLANES, align_bytes=64)
         packed = keep.tile([P, S], U8, name="packed", align_bytes=64)
-        slot_planes = [packed] + [keep.tile([P, S], U8, name=f"slot_planes{a}", align_bytes=64) for a in range(1, A)]
         nc.vector.memset(planes[:].bitcast(I32), 0)
-        for a in range(1, A):
-            nc.vector.memset(slot_planes[a][:].bitcast(I32), 0)
+
+        def interleaved(dst, src):
+            return dst.rearrange("p (c i) j -> p c j i", i=4), src.rearrange("p j (c i) -> p c j i", i=4)
 
         def quantise_pass(a):
-            x_b = keep.tile([P, T, 4], BF16, name=f"x_b{a}", align_bytes=64)
+            x_b = keep.tile([P, T, 4], BF16, name=f"x_b{a}", tag=f"x_b{a // 2}", align_bytes=64)
             cut = T - VECTOR_SHARE[a]
-            for t0, t1 in ((0, cut), (cut, T))[: 1 if cut == T else 2]:
-                dst = x_b[:, t0:t1, :].rearrange("p (c i) j -> p c j i", i=4)
-                src = x_raw[a][:, :, t0:t1].rearrange("p j (c i) -> p c j i", i=4)
-                if t0 == 0:
-                    nc.scalar.activation(out=dst, in_=src, func=ACT.Copy)
-                else:
-                    nc.vector.tensor_copy(out=dst, in_=src)
+            dst, src = interleaved(x_b[:, 0:cut, :], x_raw[a][:, :, 0:cut])
+            nc.scalar.activation(out=dst, in_=src, func=ACT.Copy)
+            dst, src = interleaved(x_b[:, cut:T, :], x_raw[a][:, :, cut:T])
+            nc.vector.tensor_copy(out=dst, in_=src)
             nc.vector.quantize_mx(
                 out=codes[:, first[a] : first[a] + T].bitcast(FP8X4),
                 scales=planes[4 * a : P, 0:T],
                 in_=x_b[:].rearrange("p c j -> p (c j)"),
             )
 
-        def gather(slots, window, e0, e1):
-            nc.vector.tensor_copy(out=slots[:, e0 * C : e1 * C], in_=window.indirect(offs_t[:, e0 * C // 16 : e1 * C // 16]))
+        def gather(dst, window, e0, e1):
+            nc.vector.tensor_copy(out=dst, in_=window.indirect(offs_t[:, e0 * C // 16 : e1 * C // 16]))
 
-        slot_codes0 = keep.tile([P, S], U32, name="slot_codes0", align_bytes=64)
+        def gather_words(dst, a, e0, e1):
+            gather(dst, codes[:, first[a] : first[a] + NARROW].bitcast(U32), e0, e1)
+
         quantise_pass(0)
-        gather(slot_codes0[:], codes[:, first[0] : first[0] + WIDE].bitcast(U32), 0, E)
+        slot_planes = [packed]
+        for a in range(1, A):
+            shifted = late.tile([P, S], U8, name=f"slot_planes{a}", offset=AT_X_FIRST + (a - 1) * S, align_bytes=64)
+            nc.vector.memset(shifted[:].bitcast(I32), 0)
+            slot_planes.append(shifted)
+        slot_first = keep.tile([P, G * C], U32, name="slot_first", align_bytes=64)
+        gather_words(slot_first[:], 0, 0, G)
         quantise_pass(1)
         quantise_pass(2)
         gather(packed[:], planes[:], 0, E)
         for a in range(1, A):
-            nc.sync.dma_start(out=slot_planes[a][0:112, :].bitcast(I32), in_=packed[4 * a : 112 + 4 * a, :].bitcast(I32))
-        w_rest = late.tile([P, 3, 4 * A, N], U8, name="w_rest", offset=8 * S, align_bytes=64)
+            nc.sync.dma_start(out=slot_planes[a][0:LIVE_ROWS, :].bitcast(I32), in_=packed[4 * a : 4 * a + LIVE_ROWS, :].bitcast(I32))
+
+        w_rest = late.tile([P, 3, G * A, N], U8, name="w_rest", offset=AT_W_REST, align_bytes=64)
         w_t = [[w_first[:], w_rest[:, 0]], [w_rest[:, 1], w_rest[:, 2]]]
-        for h, e0, e1 in ((0, 4, 8), (1, 0, 4), (1, 4, 8)):
-            load_words(w_t[h][e0 // 4], h, e0, e1)
-        slot_codes12 = late.tile([P, 2, S], U32, name="slot_codes12", offset=0, align_bytes=64)
-        slot_codes = [slot_codes0[:], slot_codes12[:, 0, :], slot_codes12[:, 1, :]]
-        for a, e0, e1 in ((1, 0, 4), (2, 0, 4), (1, 4, 8), (2, 4, 6), (2, 6, 8)):
-            gather(slot_codes[a], codes[:, first[a] : first[a] + NARROW].bitcast(U32), e0, e1)
+        for h, g in ((0, 1), (1, 0), (1, 1)):
+            load_words(w_t[h][g], h, g)
+        slot_rest = late.tile([P, 2 * A - 1, G * C], U32, name="slot_rest", offset=0, align_bytes=64)
+        slot_codes = [[slot_first[:], slot_rest[:, 0, :]]] + [[slot_rest[:, 2 * a - 1, :], slot_rest[:, 2 * a, :]] for a in range(1, A)]
+        for a in range(1, A):
+            gather_words(slot_codes[a][0], a, 0, G)
+        for a in range(A - 1):
+            gather_words(slot_codes[a][1], a, G, E)
+        last_two = E - 2
+        gather_words(slot_codes[A - 1][1][:, 0 : 2 * C], A - 1, G, last_two)
+        gather_words(slot_codes[A - 1][1][:, 2 * C : G * C], A - 1, last_two, E)
 
         wp_raw = keep.tile([P, 4, M], F32, name="wp_raw", tag="codes", align_bytes=64)
         nc.sync.dma_start(out=wp_raw[:], in_=wp.rearrange("(p j) f -> p j f", j=4))
@@ -125,46 +142,55 @@ def tile_moe_nxt_lin_relu_kernel(tc, xT, w_words, w_scales, b, wp, gate, offs, p
                 nc.tensor.transpose(spread[:, i, :], gate_in[:, k, i : i + 1].to_broadcast([P, P]), ident[:])
             nc.scalar.copy(out=gate_t[:, k, :].rearrange("m (p i) -> m p i", i=4), in_=spread[:].rearrange("m i p -> m p i"))
 
-        idle = back_pool.tile([P, N], F32, name="idle", tag="back")
-        for i in range(WARM):
-            nc.tensor.matmul_mx(
-                out=idle[:],
-                lhsT=slot_codes0[:, 0:P].bitcast(FP8X4),
-                lhsT_scale=packed[:, 0:P],
-                rhs=slot_codes0[:, 0:N].bitcast(FP8X4),
-                rhs_scale=packed[:, 0:N],
-                start=True,
-                stop=True,
-            )
-
         y = [keep.tile([P, S], F32, name=f"y{r}") for r in range(R)]
 
-        def experts(e0, e1, r):
-            acc = acc_pool.tile([P, 4, C], F32, name="acc", tag="acc")
-            for e in range(e0, e1):
-                slots = slice(e * C, (e + 1) * C)
-                for a in range(A):
-                    nc.tensor.matmul_mx(
-                        out=acc[:, e - e0, :],
-                        lhsT=w_t[r // 2][e // 4][:, e % 4 * A + a, 2 * P * (r % 2) : 2 * P * (r % 2 + 1)].bitcast(FP4X4),
-                        lhsT_scale=ws_t[:, e * A + a, P * r : P * (r + 1)],
-                        rhs=slot_codes[a][:, slots].bitcast(FP8X4),
-                        rhs_scale=slot_planes[a][:, slots],
-                        start=(a == 0),
-                        stop=(a == A - 1),
-                    )
-            for e in range(e0, e1):
-                dst = y[r][:, e * C : (e + 1) * C]
-                if e0 == 6:
-                    nc.vector.tensor_scalar(dst, acc[:, e - e0, :], b_t[:, r, e : e + 1], 0.0, ALU.add, ALU.max)
-                else:
-                    nc.scalar.activation(out=dst, in_=acc[:, e - e0, :], func=ACT.Relu, bias=b_t[:, r, e : e + 1])
+        def multiply(sums, e, r, a):
+            nc.tensor.matmul_mx(
+                out=sums,
+                lhsT=w_t[r // 2][e // G][:, e % G * A + a, 2 * P * (r % 2) : 2 * P * (r % 2 + 1)].bitcast(FP4X4),
+                lhsT_scale=ws_t[:, e * A + a, P * r : P * (r + 1)],
+                rhs=slot_codes[a][e // G][:, e % G * C : (e % G + 1) * C].bitcast(FP8X4),
+                rhs_scale=slot_planes[a][:, e * C : (e + 1) * C],
+                start=(a == 0),
+                stop=(a == A - 1),
+            )
 
-        for e0, e1, r in ((0, 4, 0), (0, 4, 1), (4, 6, 0), (6, 8, 0), (4, 8, 1), (0, 4, 2), (0, 4, 3), (4, 8, 2), (4, 8, 3)):
-            experts(e0, e1, r)
+        def activate(sums, e, r, on_vector=False):
+            dst = y[r][:, e * C : (e + 1) * C]
+            if on_vector:
+                nc.vector.tensor_scalar(dst, sums, b_t[:, r, e : e + 1], 0.0, ALU.add, ALU.max)
+            else:
+                nc.scalar.activation(out=dst, in_=sums, func=ACT.Relu, bias=b_t[:, r, e : e + 1])
+
+        def pass_by_pass(banks, e0):
+            for a in range(A):
+                for i, bank in enumerate(banks):
+                    multiply(bank[:], e0 + i % G, i // G, a)
+
+        def sum_by_sum(acc, e0, r):
+            for i in range(G):
+                for a in range(A):
+                    multiply(acc[:, i, :], e0 + i, r, a)
+            for i in range(G):
+                activate(acc[:, i, :], e0 + i, r)
+
+        banks = [acc_pool.tile([P, C], F32, name="acc", tag="acc") for i in range(4)]
+        banks = banks + [turn_pool.tile([P, C], F32, name="turned", tag="turned") for i in range(2)]
+        banks = banks + [back_pool.tile([P, C], F32, name="back", tag="back") for i in range(2)]
+        pass_by_pass(banks, 0)
+        for i, bank in enumerate(banks):
+            activate(bank[:], i % G, i // G)
+        banks = [acc_pool.tile([P, C], F32, name="acc", tag="acc") for i in range(G)]
+        pass_by_pass(banks, G)
+        for i, bank in enumerate(banks):
+            activate(bank[:], G + i, 0, on_vector=(G + i >= last_two))
+        sum_by_sum(back_pool.tile([P, G, C], F32, name="back", tag="back"), G, 1)
+        for e0 in (0, G):
+            for r in range(2, R):
+                sum_by_sum(acc_pool.tile([P, G, C], F32, name="acc", tag="acc"), e0, r)
 
         gated = [[keep.tile([P, T], F32, name=f"gated{r}_{k}") for k in range(2)] for r in range(R)]
-        c_rows = [keep.tile([P, N], BF16, name=f"c_rows{t}") for t in range(B)]
+        c_rows = keep.tile([P, B * N], BF16, name="c_rows")
 
         def fetch(r, t0, t1):
             for k in range(2):
@@ -174,49 +200,45 @@ def tile_moe_nxt_lin_relu_kernel(tc, xT, w_words, w_scales, b, wp, gate, offs, p
             for k in range(2):
                 nc.tensor.matmul(dst, lhsT=gated[r][k][:, t * P : (t + 1) * P], rhs=ident[:], is_transpose=True, start=(k == 0), stop=(k == 1))
 
-        def round_rows(t, r0, r1, sums):
-            dst = c_rows[t][:].rearrange("t (u p e) -> t u p e", u=2, e=2)[:, :, 32 * r0 : 32 * r1, :]
-            nc.scalar.copy(out=dst, in_=sums.rearrange("t (p u e) -> t u p e", u=2, e=2))
+        def round_rows(t0, t1, r, sums):
+            dst = c_rows[:, t0 * N : t1 * N].rearrange("t (b u p e) -> t b u p e", u=2, p=P, e=2)[:, :, :, 32 * r : 32 * (r + 1), :]
+            nc.scalar.copy(out=dst, in_=sums.rearrange("t (b p u e) -> t b u p e", p=32, u=2, e=2))
 
         for r in range(R - 1):
             fetch(r, 0, T)
             turned = turn_pool.tile([P, B, P], F32, name="turned", tag="turned")
             for t in range(B):
                 turn(turned[:, t, :], r, t)
-            for t in range(B):
-                round_rows(t, r, r + 1, turned[:, t, :])
+            round_rows(0, B, r, turned[:].rearrange("t b n -> t (b n)"))
 
         wp_b = late.tile([P, M, 4], BF16, name="wp_b", offset=0, align_bytes=64)
         wp_codes = keep.tile([P, M], U32, name="wp_codes", align_bytes=64)
         wp_planes = keep.tile([P, M], U8, name="wp_planes", align_bytes=64)
-        for lo, hi in ((0, 256), (256, 384)):
-            nc.scalar.activation(
-                out=wp_b[:, lo:hi, :].rearrange("p (c i) j -> p c j i", i=4),
-                in_=wp_raw[:, :, lo:hi].rearrange("p j (c i) -> p c j i", i=4),
-                func=ACT.Copy,
-            )
+        for f0, f1 in ((0, 2 * P), (2 * P, M)):
+            dst, src = interleaved(wp_b[:, f0:f1, :], wp_raw[:, :, f0:f1])
+            nc.scalar.activation(out=dst, in_=src, func=ACT.Copy)
             nc.vector.quantize_mx(
-                out=wp_codes[:, lo:hi].bitcast(FP8X4), scales=wp_planes[:, lo:hi], in_=wp_b[:, lo:hi, :].rearrange("p c j -> p (c j)")
+                out=wp_codes[:, f0:f1].bitcast(FP8X4), scales=wp_planes[:, f0:f1], in_=wp_b[:, f0:f1, :].rearrange("p c j -> p (c j)")
             )
 
-        out_rows = out.rearrange("(f p) t -> p f t", p=P)
         c_b = [keep.tile([P, 4 * P], BF16, name=f"c_b{t}", align_bytes=64) for t in range(B)]
         for t in range(B):
             turned = turn_pool.tile([P, P], F32, name="turned", tag="turned")
             fetch(R - 1, t * P, (t + 1) * P)
             turn(turned[:], R - 1, t)
-            round_rows(t, R - 1, R, turned[:])
+            round_rows(t, t + 1, R - 1, turned[:])
             back = back_pool.tile([P, 2, P], F32, name="back", tag="back")
-            pairs = c_rows[t][:].bitcast(F32)
+            pairs = c_rows[:, t * N : (t + 1) * N].bitcast(F32)
             for u in range(2):
                 nc.tensor.transpose(back[:, u, :], pairs[:, u * P : (u + 1) * P], ident[:])
             nc.scalar.copy(out=c_b[t][:].bitcast(F32).rearrange("p (t u) -> p t u", u=2), in_=back[:].rearrange("p u t -> p t u"))
 
+        out_rows = out.rearrange("(f p) t -> p f t", p=P)
         for t in range(B):
             c_codes = keep.tile([P, P], U32, name=f"c_codes{t}", align_bytes=64)
             c_planes = keep.tile([P, P], U8, name=f"c_planes{t}", align_bytes=64)
             nc.vector.quantize_mx(out=c_codes[:].bitcast(FP8X4), scales=c_planes[:], in_=c_b[t][:])
-            acc = acc_pool.tile([P, 4, C], F32, name="acc", tag="acc")
+            acc = acc_pool.tile([P, G, C], F32, name="acc", tag="acc")
             for f in range(M // P):
                 nc.tensor.matmul_mx(
                     out=acc[:, f, :],

@@ -12,12 +12,17 @@ S = E * C
 G = E // 2
 WIDE = 1376
 NARROW = 704
-VECTOR_SHARE = (352, 160, 240)
-LIVE_ROWS = 100
+VECTOR_SHARE = (352, 96, 0)
+LIVE_RUNS = ((0, 4), (32, 96), (96, 100))
+BANKS = 8
 GAP = 64
-AT_W_REST = (2 * A - 1) * G * C * 4
-AT_PLANES = AT_W_REST - 64
+AT_WP = 0
+AT_PLANES = 4 * M * 4 - 64
+AT_W_REST = 4 * M * 4
 AT_X_FIRST = AT_W_REST + 3 * G * A * N
+AT_X_LAST = AT_X_FIRST + 4 * T * 4
+AT_LATE = AT_X_LAST + 4 * T * 2
+AT_GATED = AT_LATE + 2 * P * 4 - 64
 FLOPS = 2 * K * N * E * C + 2 * N * M * T
 BYTES = 4 * K * T + E * K * N // 2 + E * K * N // 32 + 4 * N * E + 4 * N * M + 4 * 2 * T + 2 * 128 * 128 + 4 * M * T
 
@@ -38,9 +43,10 @@ def tile_moe_nxt_lin_relu_kernel(tc, xT, w_words, w_scales, b, wp, gate, offs, p
     with ExitStack() as ctx:
         keep = ctx.enter_context(tc.tile_pool(name="keep", bufs=1))
         late = ctx.enter_context(tc.tile_pool(name="late", bufs=1))
-        acc_pool = ctx.enter_context(tc.psum_pool(name="acc_pool", bufs=4))
-        turn_pool = ctx.enter_context(tc.psum_pool(name="turn_pool", bufs=2))
-        back_pool = ctx.enter_context(tc.psum_pool(name="back_pool", bufs=2))
+        psum = ctx.enter_context(tc.psum_pool(name="psum", bufs=1))
+
+        def bank(i, *shape):
+            return psum.tile([P, *shape], F32, name=f"bank{i % BANKS}", tag=f"bank{i % BANKS}")
 
         offs_t = keep.tile([P, S // 16], U16, name="offs_t")
         pos_t = [keep.tile([P, T // 16], U16, name=f"pos_t{k}") for k in range(2)]
@@ -60,6 +66,7 @@ def tile_moe_nxt_lin_relu_kernel(tc, xT, w_words, w_scales, b, wp, gate, offs, p
         nc.sync.dma_start(out=gate_in[:, :, 0:4], in_=gate[:, 0, :].rearrange("k (p i) -> p k i", i=4))
         nc.sync.dma_start(pos_t[0][:], pos1)
         nc.sync.dma_start(pos_t[1][:], pos2)
+        nc.sync.dma_start(out=b_t[:], in_=b.rearrange("(r p) e -> p r e", p=P))
 
         word_rows = w_words.rearrange("e a p c -> p (e a) c")
 
@@ -73,7 +80,6 @@ def tile_moe_nxt_lin_relu_kernel(tc, xT, w_words, w_scales, b, wp, gate, offs, p
 
         ident = keep.tile([P, P], F32, name="ident")
         make_identity(nc, ident[:])
-        nc.gpsimd.dma_start(out=b_t[:], in_=b.rearrange("(r p) e -> p r e", p=P))
 
         codes = keep.tile([P, (A - 1) * T + NARROW], I32, name="codes", tag="codes", align_bytes=64)
         nc.vector.memset(codes[:, A * T :], 0)
@@ -81,21 +87,26 @@ def tile_moe_nxt_lin_relu_kernel(tc, xT, w_words, w_scales, b, wp, gate, offs, p
         planes = late.tile([P, WIDE], U8, name="planes", offset=AT_PLANES, align_bytes=64)
         packed = keep.tile([P, S], U8, name="packed", align_bytes=64)
         nc.vector.memset(planes[:].bitcast(I32), 0)
+        plane_last = keep.tile([P, NARROW], U8, name="plane_last", align_bytes=64)
+        nc.vector.memset(plane_last[:].bitcast(I32), 0)
+        token_planes = [planes[:, 0:T], planes[4:P, 0:T], plane_last[:, 0:T]]
+        x_b = [keep.tile([P, T, 4], BF16, name=f"x_b{a}", align_bytes=64) for a in range(A - 1)]
+        x_b = x_b + [late.tile([P, T, 4], BF16, name="x_b_last", offset=AT_X_LAST, align_bytes=64)]
 
         def interleaved(dst, src):
             return dst.rearrange("p (c i) j -> p c j i", i=4), src.rearrange("p j (c i) -> p c j i", i=4)
 
         def quantise_pass(a):
-            x_b = keep.tile([P, T, 4], BF16, name=f"x_b{a}", tag=f"x_b{a // 2}", align_bytes=64)
             cut = T - VECTOR_SHARE[a]
-            dst, src = interleaved(x_b[:, 0:cut, :], x_raw[a][:, :, 0:cut])
+            dst, src = interleaved(x_b[a][:, 0:cut, :], x_raw[a][:, :, 0:cut])
             nc.scalar.activation(out=dst, in_=src, func=ACT.Copy)
-            dst, src = interleaved(x_b[:, cut:T, :], x_raw[a][:, :, cut:T])
-            nc.vector.tensor_copy(out=dst, in_=src)
+            if cut < T:
+                dst, src = interleaved(x_b[a][:, cut:T, :], x_raw[a][:, :, cut:T])
+                nc.vector.tensor_copy(out=dst, in_=src)
             nc.vector.quantize_mx(
                 out=codes[:, first[a] : first[a] + T].bitcast(FP8X4),
-                scales=planes[4 * a : P, 0:T],
-                in_=x_b[:].rearrange("p c j -> p (c j)"),
+                scales=token_planes[a],
+                in_=x_b[a][:].rearrange("p c j -> p (c j)"),
             )
 
         def gather(dst, window, e0, e1):
@@ -105,39 +116,45 @@ def tile_moe_nxt_lin_relu_kernel(tc, xT, w_words, w_scales, b, wp, gate, offs, p
             gather(dst, codes[:, first[a] : first[a] + NARROW].bitcast(U32), e0, e1)
 
         quantise_pass(0)
-        slot_planes = [packed]
-        for a in range(1, A):
-            shifted = late.tile([P, S], U8, name=f"slot_planes{a}", offset=AT_X_FIRST + (a - 1) * S, align_bytes=64)
-            nc.vector.memset(shifted[:].bitcast(I32), 0)
-            slot_planes.append(shifted)
-        slot_first = keep.tile([P, G * C], U32, name="slot_first", align_bytes=64)
-        gather_words(slot_first[:], 0, 0, G)
+        shifted = late.tile([P, S], U8, name="shifted", offset=AT_X_FIRST, align_bytes=64)
+        nc.vector.memset(shifted[:].bitcast(I32), 0)
+        slot_first = keep.tile([P, 2, G * C], U32, name="slot_first", align_bytes=64)
+        for g in range(2):
+            gather_words(slot_first[:, g, :], 0, G * g, G * (g + 1))
         quantise_pass(1)
-        quantise_pass(2)
         gather(packed[:], planes[:], 0, E)
-        for a in range(1, A):
-            nc.sync.dma_start(out=slot_planes[a][0:LIVE_ROWS, :].bitcast(I32), in_=packed[4 * a : 4 * a + LIVE_ROWS, :].bitcast(I32))
+        for lo, hi in LIVE_RUNS:
+            nc.sync.dma_start(out=shifted[lo:hi, :].bitcast(I32), in_=packed[4 + lo : 4 + hi, :].bitcast(I32))
 
         w_rest = late.tile([P, 3, G * A, N], U8, name="w_rest", offset=AT_W_REST, align_bytes=64)
         w_t = [[w_first[:], w_rest[:, 0]], [w_rest[:, 1], w_rest[:, 2]]]
-        for h, g in ((0, 1), (1, 0), (1, 1)):
-            load_words(w_t[h][g], h, g)
-        slot_rest = late.tile([P, 2 * A - 1, G * C], U32, name="slot_rest", offset=0, align_bytes=64)
-        slot_codes = [[slot_first[:], slot_rest[:, 0, :]]] + [[slot_rest[:, 2 * a - 1, :], slot_rest[:, 2 * a, :]] for a in range(1, A)]
-        for a in range(1, A):
-            gather_words(slot_codes[a][0], a, 0, G)
-        for a in range(A - 1):
-            gather_words(slot_codes[a][1], a, G, E)
-        last_two = E - 2
-        gather_words(slot_codes[A - 1][1][:, 0 : 2 * C], A - 1, G, last_two)
-        gather_words(slot_codes[A - 1][1][:, 2 * C : G * C], A - 1, last_two, E)
-
-        wp_raw = keep.tile([P, 4, M], F32, name="wp_raw", tag="codes", align_bytes=64)
+        wp_raw = late.tile([P, 4, M], F32, name="wp_raw", offset=AT_WP, align_bytes=64)
+        load_words(w_t[0][1], 0, 1)
         nc.sync.dma_start(out=wp_raw[:], in_=wp.rearrange("(p j) f -> p j f", j=4))
+        for g in range(2):
+            load_words(w_t[1][g], 1, g)
+        slot_rest = keep.tile([P, 3, G * C], U32, name="slot_rest", align_bytes=64)
+        gather_words(slot_rest[:, 0, :], 1, 0, G)
+        quantise_pass(2)
+        slot_last = keep.tile([P, S], U8, name="slot_last", align_bytes=64)
+        slot_planes = [packed, shifted, slot_last]
+        gather(slot_last[:, 0 : G * C], plane_last[:], 0, G)
+        gather_words(slot_rest[:, 1, :], 2, 0, G)
+        slot_mid = late.tile([P, G * C], U32, name="slot_mid", offset=AT_X_LAST, align_bytes=64)
+        gather_words(slot_mid[:], 1, G, E)
+        gather(slot_last[:, G * C : S], plane_last[:], G, E)
+        last_two = E - 2
+        gather_words(slot_rest[:, 2, 0 : 2 * C], 2, G, last_two)
+        gather_words(slot_rest[:, 2, 2 * C : G * C], 2, last_two, E)
+        slot_codes = [[slot_first[:, 0, :], slot_first[:, 1, :]], [slot_rest[:, 0, :], slot_mid[:]], [slot_rest[:, 1, :], slot_rest[:, 2, :]]]
+
+        wp_b = keep.tile([P, M, 4], BF16, name="wp_b", tag="codes", align_bytes=64)
+        dst, src = interleaved(wp_b[:], wp_raw[:])
+        nc.vector.tensor_copy(out=dst, in_=src)
 
         gate_t = keep.tile([P, 2, T], F32, name="gate_t")
         for k in range(2):
-            spread = turn_pool.tile([P, 4, P], F32, name="spread", tag="turned")
+            spread = bank(BANKS - 2 + k, 4, P)
             for i in range(4):
                 nc.tensor.transpose(spread[:, i, :], gate_in[:, k, i : i + 1].to_broadcast([P, P]), ident[:])
             nc.scalar.copy(out=gate_t[:, k, :].rearrange("m (p i) -> m p i", i=4), in_=spread[:].rearrange("m i p -> m p i"))
@@ -155,93 +172,101 @@ def tile_moe_nxt_lin_relu_kernel(tc, xT, w_words, w_scales, b, wp, gate, offs, p
                 stop=(a == A - 1),
             )
 
-        def activate(sums, e, r, on_vector=False):
-            dst = y[r][:, e * C : (e + 1) * C]
-            if on_vector:
-                nc.vector.tensor_scalar(dst, sums, b_t[:, r, e : e + 1], 0.0, ALU.add, ALU.max)
-            else:
-                nc.scalar.activation(out=dst, in_=sums, func=ACT.Relu, bias=b_t[:, r, e : e + 1])
+        def activate(sums, e, r):
+            nc.scalar.activation(out=y[r][:, e * C : (e + 1) * C], in_=sums, func=ACT.Relu, bias=b_t[:, r, e : e + 1])
 
-        def pass_by_pass(banks, e0):
-            for a in range(A):
-                for i, bank in enumerate(banks):
-                    multiply(bank[:], e0 + i % G, i // G, a)
-
-        def sum_by_sum(acc, e0, r):
-            for i in range(G):
+        def sum_by_sum(at, e0, e1, r):
+            acc = bank(at, e1 - e0, C)
+            for e in range(e0, e1):
                 for a in range(A):
-                    multiply(acc[:, i, :], e0 + i, r, a)
-            for i in range(G):
-                activate(acc[:, i, :], e0 + i, r)
+                    multiply(acc[:, e - e0, :], e, r, a)
+            for e in range(e0, e1):
+                activate(acc[:, e - e0, :], e, r)
 
-        banks = [acc_pool.tile([P, C], F32, name="acc", tag="acc") for i in range(4)]
-        banks = banks + [turn_pool.tile([P, C], F32, name="turned", tag="turned") for i in range(2)]
-        banks = banks + [back_pool.tile([P, C], F32, name="back", tag="back") for i in range(2)]
-        pass_by_pass(banks, 0)
-        for i, bank in enumerate(banks):
-            activate(bank[:], i % G, i // G)
-        banks = [acc_pool.tile([P, C], F32, name="acc", tag="acc") for i in range(G)]
-        pass_by_pass(banks, G)
-        for i, bank in enumerate(banks):
-            activate(bank[:], G + i, 0, on_vector=(G + i >= last_two))
-        sum_by_sum(back_pool.tile([P, G, C], F32, name="back", tag="back"), G, 1)
-        for e0 in (0, G):
-            for r in range(2, R):
-                sum_by_sum(acc_pool.tile([P, G, C], F32, name="acc", tag="acc"), e0, r)
+        def pass_by_pass(sums, e0):
+            open_sums = [bank(i, C) for i in range(sums)]
+            for a in range(A):
+                for i in range(sums):
+                    multiply(open_sums[i][:], e0 + i % G, i // G, a)
+            for i in range(sums):
+                activate(open_sums[i][:], e0 + i % G, i // G)
 
-        gated = [[keep.tile([P, T], F32, name=f"gated{r}_{k}") for k in range(2)] for r in range(R)]
+        pass_by_pass(BANKS, 0)
+        pass_by_pass(G, G)
+        sum_by_sum(4, G, last_two, 1)
+        sum_by_sum(5, last_two, E, 1)
+        sum_by_sum(6, 0, G, 2)
+        sum_by_sum(0, G, last_two, 2)
+        sum_by_sum(1, last_two, E, 2)
+        sum_by_sum(2, 0, G, 3)
+        sum_by_sum(3, G, last_two, 3)
+        sum_by_sum(4, last_two, E, 3)
+
+        gated = [[late.tile([P, T], F32, name="gated0_0", offset=AT_WP, align_bytes=64), keep.tile([P, T], F32, name="gated0_1")]]
+        gated = gated + [[late.tile([P, T], F32, name=f"gated1_{k}", offset=AT_GATED + k * T * 4, align_bytes=64) for k in range(2)]]
+        early_half = [[keep.tile([P, 2 * P], F32, name=f"early{r}_{k}") for k in range(2)] for r in range(2, R)]
+        late_half = [[late.tile([P, 2 * P], F32, name=f"late{r}_{k}", offset=AT_LATE + (2 * k + r - 2) * 2 * P * 4, align_bytes=64) for k in range(2)] for r in range(2, R)]
+
+        def product(r, k, t0, t1):
+            if r < 2:
+                return gated[r][k][:, t0:t1]
+            if t0 < 2 * P:
+                return early_half[r - 2][k][:, t0:t1]
+            return late_half[r - 2][k][:, t0 - 2 * P : t1 - 2 * P]
+
         c_rows = keep.tile([P, B * N], BF16, name="c_rows")
 
         def fetch(r, t0, t1):
             for k in range(2):
-                nc.vector.tensor_tensor(gated[r][k][:, t0:t1], y[r][:].indirect(pos_t[k][:, t0 // 16 : t1 // 16]), gate_t[:, k, t0:t1], ALU.mult)
+                nc.vector.tensor_tensor(product(r, k, t0, t1), y[r][:].indirect(pos_t[k][:, t0 // 16 : t1 // 16]), gate_t[:, k, t0:t1], ALU.mult)
 
         def turn(dst, r, t):
             for k in range(2):
-                nc.tensor.matmul(dst, lhsT=gated[r][k][:, t * P : (t + 1) * P], rhs=ident[:], is_transpose=True, start=(k == 0), stop=(k == 1))
+                nc.tensor.matmul(dst, lhsT=product(r, k, t * P, (t + 1) * P), rhs=ident[:], is_transpose=True, start=(k == 0), stop=(k == 1))
 
-        def round_rows(t0, t1, r, sums):
-            dst = c_rows[:, t0 * N : t1 * N].rearrange("t (b u p e) -> t b u p e", u=2, p=P, e=2)[:, :, :, 32 * r : 32 * (r + 1), :]
-            nc.scalar.copy(out=dst, in_=sums.rearrange("t (b p u e) -> t b u p e", p=32, u=2, e=2))
+        def round_rows(t0, t1, r0, r1, sums):
+            dst = c_rows[:, t0 * N : t1 * N].rearrange("t (b u p e) -> t b u p e", u=2, p=P, e=2)[:, :, :, 32 * r0 : 32 * r1, :]
+            nc.scalar.copy(out=dst, in_=sums.rearrange("t (b p u e) -> t b u p e", p=32 * (r1 - r0), u=2, e=2))
 
-        for r in range(R - 1):
+        for r in range(2):
             fetch(r, 0, T)
-            turned = turn_pool.tile([P, B, P], F32, name="turned", tag="turned")
+            turned = bank(3 + r, B, P)
             for t in range(B):
                 turn(turned[:, t, :], r, t)
-            round_rows(0, B, r, turned[:].rearrange("t b n -> t (b n)"))
+            round_rows(0, B, r, r + 1, turned[:].rearrange("t b n -> t (b n)"))
 
-        wp_b = late.tile([P, M, 4], BF16, name="wp_b", offset=0, align_bytes=64)
         wp_codes = keep.tile([P, M], U32, name="wp_codes", align_bytes=64)
-        wp_planes = keep.tile([P, M], U8, name="wp_planes", align_bytes=64)
-        for f0, f1 in ((0, 2 * P), (2 * P, M)):
-            dst, src = interleaved(wp_b[:, f0:f1, :], wp_raw[:, :, f0:f1])
-            nc.scalar.activation(out=dst, in_=src, func=ACT.Copy)
-            nc.vector.quantize_mx(
-                out=wp_codes[:, f0:f1].bitcast(FP8X4), scales=wp_planes[:, f0:f1], in_=wp_b[:, f0:f1, :].rearrange("p c j -> p (c j)")
-            )
+        wp_planes = late.tile([P, M], U8, name="wp_planes", offset=AT_LATE + 4 * 2 * P * 4, align_bytes=64)
 
         c_b = [keep.tile([P, 4 * P], BF16, name=f"c_b{t}", align_bytes=64) for t in range(B)]
         for t in range(B):
-            turned = turn_pool.tile([P, P], F32, name="turned", tag="turned")
-            fetch(R - 1, t * P, (t + 1) * P)
-            turn(turned[:], R - 1, t)
-            round_rows(t, t + 1, R - 1, turned[:])
-            back = back_pool.tile([P, 2, P], F32, name="back", tag="back")
+            if t % 2 == 0:
+                fetch(2, t * P, (t + 2) * P)
+            fetch(3, t * P, (t + 1) * P)
+            turned = bank(t % 2, 2, P)
+            for r in range(2, R):
+                turn(turned[:, r - 2, :], r, t)
+            round_rows(t, t + 1, 2, R, turned[:].rearrange("t r n -> t (r n)"))
+            back = bank(2 + t % 2, 2, P)
             pairs = c_rows[:, t * N : (t + 1) * N].bitcast(F32)
             for u in range(2):
                 nc.tensor.transpose(back[:, u, :], pairs[:, u * P : (u + 1) * P], ident[:])
             nc.scalar.copy(out=c_b[t][:].bitcast(F32).rearrange("p (t u) -> p t u", u=2), in_=back[:].rearrange("p u t -> p t u"))
+
+        for f0, f1 in ((0, 2 * P), (2 * P, M)):
+            nc.vector.quantize_mx(
+                out=wp_codes[:, f0:f1].bitcast(FP8X4), scales=wp_planes[:, f0:f1], in_=wp_b[:, f0:f1, :].rearrange("p c j -> p (c j)")
+            )
 
         out_rows = out.rearrange("(f p) t -> p f t", p=P)
         for t in range(B):
             c_codes = keep.tile([P, P], U32, name=f"c_codes{t}", align_bytes=64)
             c_planes = keep.tile([P, P], U8, name=f"c_planes{t}", align_bytes=64)
             nc.vector.quantize_mx(out=c_codes[:].bitcast(FP8X4), scales=c_planes[:], in_=c_b[t][:])
-            acc = acc_pool.tile([P, G, C], F32, name="acc", tag="acc")
+            sums = [bank(4 + 2 * (t % 2), 2, P), bank(5 + 2 * (t % 2), 1, P)]
             for f in range(M // P):
                 nc.tensor.matmul_mx(
-                    out=acc[:, f, :],
+                    out=sums[f // 2][:, f % 2, :],
                     lhsT=wp_codes[:, f * P : (f + 1) * P].bitcast(FP8X4),
                     lhsT_scale=wp_planes[:, f * P : (f + 1) * P],
                     rhs=c_codes[:].bitcast(FP8X4),
@@ -249,9 +274,7 @@ def tile_moe_nxt_lin_relu_kernel(tc, xT, w_words, w_scales, b, wp, gate, offs, p
                     start=True,
                     stop=True,
                 )
-            result = keep.tile([P, M // P, P + GAP // 4], F32, name=f"result{t}")[:, :, 0:P]
-            if t % 2 == 0:
-                nc.scalar.copy(out=result, in_=acc[:, 0 : M // P, :])
-            else:
-                nc.vector.tensor_copy(out=result, in_=acc[:, 0 : M // P, :])
-            nc.sync.dma_start(out=out_rows[:, :, t * P : (t + 1) * P], in_=result)
+            result = keep.tile([P, M // P, P + GAP // 4], F32, name=f"result{t}")
+            nc.scalar.copy(out=result[:, 0:2, 0:P], in_=sums[0][:])
+            nc.vector.tensor_copy(out=result[:, 2:3, 0:P], in_=sums[1][:])
+            nc.sync.dma_start(out=out_rows[:, :, t * P : (t + 1) * P], in_=result[:, :, 0:P])

@@ -12,16 +12,14 @@ S = E * C
 G = E // 2
 WIDE = 1376
 NARROW = 704
-VECTOR_SHARE = (352, 96, 0)
+VECTOR_SHARE = (352, 0, 240)
 LIVE_RUNS = ((0, 4), (32, 96), (96, 100))
 BANKS = 8
 GAP = 64
-AT_WP = 0
-AT_PLANES = 4 * M * 4 - 64
-AT_W_REST = 4 * M * 4
+AT_W_REST = 4 * G * C * 4
+AT_PLANES = AT_W_REST - 64
 AT_X_FIRST = AT_W_REST + 3 * G * A * N
-AT_X_LAST = AT_X_FIRST + 4 * T * 4
-AT_LATE = AT_X_LAST + 4 * T * 2
+AT_LATE = AT_X_FIRST + 4 * T * 4
 AT_GATED = AT_LATE + 2 * P * 4 - 64
 FLOPS = 2 * K * N * E * C + 2 * N * M * T
 BYTES = 4 * K * T + E * K * N // 2 + E * K * N // 32 + 4 * N * E + 4 * N * M + 4 * 2 * T + 2 * 128 * 128 + 4 * M * T
@@ -87,11 +85,7 @@ def tile_moe_nxt_lin_relu_kernel(tc, xT, w_words, w_scales, b, wp, gate, offs, p
         planes = late.tile([P, WIDE], U8, name="planes", offset=AT_PLANES, align_bytes=64)
         packed = keep.tile([P, S], U8, name="packed", align_bytes=64)
         nc.vector.memset(planes[:].bitcast(I32), 0)
-        plane_last = keep.tile([P, NARROW], U8, name="plane_last", align_bytes=64)
-        nc.vector.memset(plane_last[:].bitcast(I32), 0)
-        token_planes = [planes[:, 0:T], planes[4:P, 0:T], plane_last[:, 0:T]]
-        x_b = [keep.tile([P, T, 4], BF16, name=f"x_b{a}", align_bytes=64) for a in range(A - 1)]
-        x_b = x_b + [late.tile([P, T, 4], BF16, name="x_b_last", offset=AT_X_LAST, align_bytes=64)]
+        x_b = [keep.tile([P, T, 4], BF16, name=f"x_b{a}", align_bytes=64) for a in range(A)]
 
         def interleaved(dst, src):
             return dst.rearrange("p (c i) j -> p c j i", i=4), src.rearrange("p j (c i) -> p c j i", i=4)
@@ -105,7 +99,7 @@ def tile_moe_nxt_lin_relu_kernel(tc, xT, w_words, w_scales, b, wp, gate, offs, p
                 nc.vector.tensor_copy(out=dst, in_=src)
             nc.vector.quantize_mx(
                 out=codes[:, first[a] : first[a] + T].bitcast(FP8X4),
-                scales=token_planes[a],
+                scales=planes[4 * a : P, 0:T],
                 in_=x_b[a][:].rearrange("p c j -> p (c j)"),
             )
 
@@ -116,41 +110,35 @@ def tile_moe_nxt_lin_relu_kernel(tc, xT, w_words, w_scales, b, wp, gate, offs, p
             gather(dst, codes[:, first[a] : first[a] + NARROW].bitcast(U32), e0, e1)
 
         quantise_pass(0)
-        shifted = late.tile([P, S], U8, name="shifted", offset=AT_X_FIRST, align_bytes=64)
+        shifted = late.tile([P, A - 1, S], U8, name="shifted", offset=AT_X_FIRST, align_bytes=64)
         nc.vector.memset(shifted[:].bitcast(I32), 0)
+        slot_planes = [packed[:], shifted[:, 0, :], shifted[:, 1, :]]
         slot_first = keep.tile([P, 2, G * C], U32, name="slot_first", align_bytes=64)
         for g in range(2):
             gather_words(slot_first[:, g, :], 0, G * g, G * (g + 1))
         quantise_pass(1)
+        quantise_pass(2)
         gather(packed[:], planes[:], 0, E)
-        for lo, hi in LIVE_RUNS:
-            nc.sync.dma_start(out=shifted[lo:hi, :].bitcast(I32), in_=packed[4 + lo : 4 + hi, :].bitcast(I32))
+        for a in range(1, A):
+            for lo, hi in LIVE_RUNS:
+                nc.sync.dma_start(out=slot_planes[a][lo:hi, :].bitcast(I32), in_=packed[4 * a + lo : 4 * a + hi, :].bitcast(I32))
 
         w_rest = late.tile([P, 3, G * A, N], U8, name="w_rest", offset=AT_W_REST, align_bytes=64)
         w_t = [[w_first[:], w_rest[:, 0]], [w_rest[:, 1], w_rest[:, 2]]]
-        wp_raw = late.tile([P, 4, M], F32, name="wp_raw", offset=AT_WP, align_bytes=64)
-        load_words(w_t[0][1], 0, 1)
-        nc.sync.dma_start(out=wp_raw[:], in_=wp.rearrange("(p j) f -> p j f", j=4))
-        for g in range(2):
-            load_words(w_t[1][g], 1, g)
-        slot_rest = keep.tile([P, 3, G * C], U32, name="slot_rest", align_bytes=64)
-        gather_words(slot_rest[:, 0, :], 1, 0, G)
-        quantise_pass(2)
-        slot_last = keep.tile([P, S], U8, name="slot_last", align_bytes=64)
-        slot_planes = [packed, shifted, slot_last]
-        gather(slot_last[:, 0 : G * C], plane_last[:], 0, G)
-        gather_words(slot_rest[:, 1, :], 2, 0, G)
-        slot_mid = late.tile([P, G * C], U32, name="slot_mid", offset=AT_X_LAST, align_bytes=64)
-        gather_words(slot_mid[:], 1, G, E)
-        gather(slot_last[:, G * C : S], plane_last[:], G, E)
+        for h, g in ((0, 1), (1, 0), (1, 1)):
+            load_words(w_t[h][g], h, g)
+        slot_rest = late.tile([P, 2, 2, G * C], U32, name="slot_rest", offset=0, align_bytes=64)
+        slot_codes = [slot_first[:], slot_rest[:, 0], slot_rest[:, 1]]
+        for a in range(1, A):
+            gather_words(slot_codes[a][:, 0, :], a, 0, G)
+        gather_words(slot_codes[1][:, 1, :], 1, G, E)
         last_two = E - 2
-        gather_words(slot_rest[:, 2, 0 : 2 * C], 2, G, last_two)
-        gather_words(slot_rest[:, 2, 2 * C : G * C], 2, last_two, E)
-        slot_codes = [[slot_first[:, 0, :], slot_first[:, 1, :]], [slot_rest[:, 0, :], slot_mid[:]], [slot_rest[:, 1, :], slot_rest[:, 2, :]]]
+        gather_words(slot_codes[2][:, 1, 0 : 2 * C], 2, G, last_two)
+        gather_words(slot_codes[2][:, 1, 2 * C : 3 * C], 2, last_two, E - 1)
+        gather_words(slot_codes[2][:, 1, 3 * C : G * C], 2, E - 1, E)
 
-        wp_b = keep.tile([P, M, 4], BF16, name="wp_b", tag="codes", align_bytes=64)
-        dst, src = interleaved(wp_b[:], wp_raw[:])
-        nc.vector.tensor_copy(out=dst, in_=src)
+        wp_raw = keep.tile([P, 4, M], F32, name="wp_raw", tag="codes", align_bytes=64)
+        nc.sync.dma_start(out=wp_raw[:], in_=wp.rearrange("(p j) f -> p j f", j=4))
 
         gate_t = keep.tile([P, 2, T], F32, name="gate_t")
         for k in range(2):
@@ -166,14 +154,18 @@ def tile_moe_nxt_lin_relu_kernel(tc, xT, w_words, w_scales, b, wp, gate, offs, p
                 out=sums,
                 lhsT=w_t[r // 2][e // G][:, e % G * A + a, 2 * P * (r % 2) : 2 * P * (r % 2 + 1)].bitcast(FP4X4),
                 lhsT_scale=ws_t[:, e * A + a, P * r : P * (r + 1)],
-                rhs=slot_codes[a][e // G][:, e % G * C : (e % G + 1) * C].bitcast(FP8X4),
+                rhs=slot_codes[a][:, e // G, e % G * C : (e % G + 1) * C].bitcast(FP8X4),
                 rhs_scale=slot_planes[a][:, e * C : (e + 1) * C],
                 start=(a == 0),
                 stop=(a == A - 1),
             )
 
-        def activate(sums, e, r):
-            nc.scalar.activation(out=y[r][:, e * C : (e + 1) * C], in_=sums, func=ACT.Relu, bias=b_t[:, r, e : e + 1])
+        def activate(sums, e, r, on_vector=False):
+            dst = y[r][:, e * C : (e + 1) * C]
+            if on_vector:
+                nc.vector.tensor_scalar(dst, sums, b_t[:, r, e : e + 1], 0.0, ALU.add, ALU.max)
+            else:
+                nc.scalar.activation(out=dst, in_=sums, func=ACT.Relu, bias=b_t[:, r, e : e + 1])
 
         def sum_by_sum(at, e0, e1, r):
             acc = bank(at, e1 - e0, C)
@@ -183,26 +175,28 @@ def tile_moe_nxt_lin_relu_kernel(tc, xT, w_words, w_scales, b, wp, gate, offs, p
             for e in range(e0, e1):
                 activate(acc[:, e - e0, :], e, r)
 
-        def pass_by_pass(sums, e0):
-            open_sums = [bank(i, C) for i in range(sums)]
+        for e0 in (0, G):
+            open_sums = [bank(e0 + i, C) for i in range(G)]
             for a in range(A):
-                for i in range(sums):
-                    multiply(open_sums[i][:], e0 + i % G, i // G, a)
-            for i in range(sums):
-                activate(open_sums[i][:], e0 + i % G, i // G)
-
-        pass_by_pass(BANKS, 0)
-        pass_by_pass(G, G)
-        sum_by_sum(4, G, last_two, 1)
-        sum_by_sum(5, last_two, E, 1)
-        sum_by_sum(6, 0, G, 2)
+                for i in range(G):
+                    multiply(open_sums[i][:], e0 + i, 0, a)
+            for i in range(G):
+                activate(open_sums[i][:], e0 + i, 0, on_vector=(e0 + i == E - 1))
+        sum_by_sum(4, 0, G, 1)
+        sum_by_sum(5, G, last_two, 1)
+        sum_by_sum(6, last_two, E, 1)
+        sum_by_sum(7, 0, G, 2)
         sum_by_sum(0, G, last_two, 2)
         sum_by_sum(1, last_two, E, 2)
         sum_by_sum(2, 0, G, 3)
         sum_by_sum(3, G, last_two, 3)
         sum_by_sum(4, last_two, E, 3)
 
-        gated = [[late.tile([P, T], F32, name="gated0_0", offset=AT_WP, align_bytes=64), keep.tile([P, T], F32, name="gated0_1")]]
+        wp_b = late.tile([P, M, 4], BF16, name="wp_b", offset=0, align_bytes=64)
+        dst, src = interleaved(wp_b[:], wp_raw[:])
+        nc.scalar.activation(out=dst, in_=src, func=ACT.Copy)
+
+        gated = [[keep.tile([P, T], F32, name=f"gated0_{k}") for k in range(2)]]
         gated = gated + [[late.tile([P, T], F32, name=f"gated1_{k}", offset=AT_GATED + k * T * 4, align_bytes=64) for k in range(2)]]
         early_half = [[keep.tile([P, 2 * P], F32, name=f"early{r}_{k}") for k in range(2)] for r in range(2, R)]
         late_half = [[late.tile([P, 2 * P], F32, name=f"late{r}_{k}", offset=AT_LATE + (2 * k + r - 2) * 2 * P * 4, align_bytes=64) for k in range(2)] for r in range(2, R)]

@@ -10,17 +10,22 @@ R = N // P
 B = T // P
 S = E * C
 G = E // 2
-WIDE = 1376
-NARROW = 704
-VECTOR_SHARE = (352, 0, 240)
-LIVE_RUNS = ((0, 4), (32, 96), (96, 100))
+HALF = N // 2
 BANKS = 8
+WIDE = 1408
+MIDDLE = 1024
+NARROW = 704
+VECTOR_SHARE = (352, 0, 128)
+LIVE_RUNS = ((0, 4), (32, 96), (96, 100))
 GAP = 64
-AT_W_REST = 4 * G * C * 4
-AT_PLANES = AT_W_REST - 64
-AT_X_FIRST = AT_W_REST + 3 * G * A * N
-AT_LATE = AT_X_FIRST + 4 * T * 4
-AT_GATED = AT_LATE + 2 * P * 4 - 64
+WS_BYTES = E * A * (HALF + GAP)
+LAP = 64
+AT_PLANES = (2 * E - 2) * C * 4 - LAP
+AT_WS_REST = AT_PLANES + WIDE
+AT_W_REST = AT_WS_REST + WS_BYTES
+AT_X_FIRST = AT_W_REST + E * A * N
+AT_LAST = AT_X_FIRST + 4 * T * 4
+AT_GATED = AT_LAST + P * 4 - LAP
 FLOPS = 2 * K * N * E * C + 2 * N * M * T
 BYTES = 4 * K * T + E * K * N // 2 + E * K * N // 32 + 4 * N * E + 4 * N * M + 4 * 2 * T + 2 * 128 * 128 + 4 * M * T
 
@@ -44,18 +49,18 @@ def tile_moe_nxt_lin_relu_kernel(tc, xT, w_words, w_scales, b, wp, gate, offs, p
         psum = ctx.enter_context(tc.psum_pool(name="psum", bufs=1))
 
         def bank(i, *shape):
-            return psum.tile([P, *shape], F32, name=f"bank{i % BANKS}", tag=f"bank{i % BANKS}")
+            return psum.tile([P, *shape], F32, name=f"bank{i}", tag=f"bank{i}")
 
         offs_t = keep.tile([P, S // 16], U16, name="offs_t")
         pos_t = [keep.tile([P, T // 16], U16, name=f"pos_t{k}") for k in range(2)]
         x_raw = [late.tile([P, 4, T], F32, name="x_raw0", offset=AT_X_FIRST, align_bytes=64)]
         x_raw = x_raw + [keep.tile([P, 4, T], F32, name=f"x_raw{a}") for a in range(1, A)]
-        w_first = keep.tile([P, G * A, N], U8, name="w_first", align_bytes=64)
-        ws_t = keep.tile([P, E * A, N + GAP], U8, name="ws_t", align_bytes=64)
+        w_first = keep.tile([P, E * A, N], U8, name="w_first", align_bytes=64)
+        ws_first = keep.tile([P, E * A, HALF + GAP], U8, name="ws_first", align_bytes=64)
         b_t = keep.tile([P, R, E], F32, name="b_t")
         gate_in = keep.tile([P, 2, 8], F32, name="gate_in")
 
-        nc.vector.memset(ws_t[:, :, 0:N].bitcast(I32), 0)
+        nc.vector.memset(ws_first[:, :, 0:HALF].bitcast(I32), 0)
 
         for a in range(A):
             nc.sync.dma_start(out=x_raw[a][:], in_=xT[512 * a : 512 * (a + 1), :].rearrange("(p j) t -> p j t", j=4))
@@ -68,13 +73,18 @@ def tile_moe_nxt_lin_relu_kernel(tc, xT, w_words, w_scales, b, wp, gate, offs, p
 
         word_rows = w_words.rearrange("e a p c -> p (e a) c")
 
-        def load_words(dst, h, g):
-            nc.sync.dma_start(out=dst.bitcast(I32), in_=word_rows[:, G * A * g : G * A * (g + 1), N * h : N * (h + 1)].bitcast(I32))
+        def load_words(dst, h, e0, e1):
+            nc.sync.dma_start(out=dst.bitcast(I32), in_=word_rows[:, A * e0 : A * e1, N * h : N * (h + 1)].bitcast(I32))
 
-        load_words(w_first[:], 0, 0)
         scale_rows = w_scales.rearrange("e a q n -> q (e a) n")
-        for i in range(4):
-            nc.sync.dma_start(out=ws_t[i:P:32, :, 0:N].bitcast(I32), in_=scale_rows[i:16:4, :, :].bitcast(I32))
+
+        def load_scales(dst, h):
+            for i in range(4):
+                nc.sync.dma_start(out=dst[i:P:32, :, 0:HALF].bitcast(I32), in_=scale_rows[i:16:4, :, HALF * h : HALF * (h + 1)].bitcast(I32))
+
+        load_scales(ws_first, 0)
+        for g in range(2):
+            load_words(w_first[:, G * A * g : G * A * (g + 1), :], 0, G * g, G * (g + 1))
 
         ident = keep.tile([P, P], F32, name="ident")
         make_identity(nc, ident[:])
@@ -82,7 +92,7 @@ def tile_moe_nxt_lin_relu_kernel(tc, xT, w_words, w_scales, b, wp, gate, offs, p
         codes = keep.tile([P, (A - 1) * T + NARROW], I32, name="codes", tag="codes", align_bytes=64)
         nc.vector.memset(codes[:, A * T :], 0)
         first = [(A - 1 - a) * T for a in range(A)]
-        planes = late.tile([P, WIDE], U8, name="planes", offset=AT_PLANES, align_bytes=64)
+        planes = late.tile([P, WIDE + WS_BYTES + LAP], U8, name="planes", offset=AT_PLANES, align_bytes=64)
         packed = keep.tile([P, S], U8, name="packed", align_bytes=64)
         nc.vector.memset(planes[:].bitcast(I32), 0)
         x_b = [keep.tile([P, T, 4], BF16, name=f"x_b{a}", align_bytes=64) for a in range(A)]
@@ -90,52 +100,65 @@ def tile_moe_nxt_lin_relu_kernel(tc, xT, w_words, w_scales, b, wp, gate, offs, p
         def interleaved(dst, src):
             return dst.rearrange("p (c i) j -> p c j i", i=4), src.rearrange("p j (c i) -> p c j i", i=4)
 
-        def quantise_pass(a):
+        def interleave_pass(a):
             cut = T - VECTOR_SHARE[a]
             dst, src = interleaved(x_b[a][:, 0:cut, :], x_raw[a][:, :, 0:cut])
             nc.scalar.activation(out=dst, in_=src, func=ACT.Copy)
             if cut < T:
                 dst, src = interleaved(x_b[a][:, cut:T, :], x_raw[a][:, :, cut:T])
                 nc.vector.tensor_copy(out=dst, in_=src)
+
+        def quantise_pass(a):
             nc.vector.quantize_mx(
                 out=codes[:, first[a] : first[a] + T].bitcast(FP8X4),
                 scales=planes[4 * a : P, 0:T],
                 in_=x_b[a][:].rearrange("p c j -> p (c j)"),
             )
 
+        ahead = S + 2 * C
+        slot_first = keep.tile([P, ahead], U32, name="slot_first", align_bytes=64)
+        slot_rest = late.tile([P, A * S - ahead], U32, name="slot_rest", offset=0, align_bytes=64)
+
+        def slot_words(a, e0, e1):
+            lo, hi = a * S + e0 * C, a * S + e1 * C
+            return slot_first[:, lo:hi] if lo < ahead else slot_rest[:, lo - ahead : hi - ahead]
+
         def gather(dst, window, e0, e1):
             nc.vector.tensor_copy(out=dst, in_=window.indirect(offs_t[:, e0 * C // 16 : e1 * C // 16]))
 
-        def gather_words(dst, a, e0, e1):
-            gather(dst, codes[:, first[a] : first[a] + NARROW].bitcast(U32), e0, e1)
+        def gather_words(a, e0, e1, width=NARROW):
+            gather(slot_words(a, e0, e1), codes[:, first[a] : first[a] + width].bitcast(U32), e0, e1)
 
+        interleave_pass(0)
         quantise_pass(0)
         shifted = late.tile([P, A - 1, S], U8, name="shifted", offset=AT_X_FIRST, align_bytes=64)
         nc.vector.memset(shifted[:].bitcast(I32), 0)
         slot_planes = [packed[:], shifted[:, 0, :], shifted[:, 1, :]]
-        slot_first = keep.tile([P, 2, G * C], U32, name="slot_first", align_bytes=64)
         for g in range(2):
-            gather_words(slot_first[:, g, :], 0, G * g, G * (g + 1))
+            gather_words(0, G * g, G * (g + 1))
+        interleave_pass(1)
         quantise_pass(1)
+        interleave_pass(2)
+        gather_words(1, 0, 2)
         quantise_pass(2)
-        gather(packed[:], planes[:], 0, E)
+        gather(packed[:], planes[:, 0:WIDE], 0, E)
         for a in range(1, A):
             for lo, hi in LIVE_RUNS:
                 nc.sync.dma_start(out=slot_planes[a][lo:hi, :].bitcast(I32), in_=packed[4 * a + lo : 4 * a + hi, :].bitcast(I32))
 
-        w_rest = late.tile([P, 3, G * A, N], U8, name="w_rest", offset=AT_W_REST, align_bytes=64)
-        w_t = [[w_first[:], w_rest[:, 0]], [w_rest[:, 1], w_rest[:, 2]]]
-        for h, g in ((0, 1), (1, 0), (1, 1)):
-            load_words(w_t[h][g], h, g)
-        slot_rest = late.tile([P, 2, 2, G * C], U32, name="slot_rest", offset=0, align_bytes=64)
-        slot_codes = [slot_first[:], slot_rest[:, 0], slot_rest[:, 1]]
-        for a in range(1, A):
-            gather_words(slot_codes[a][:, 0, :], a, 0, G)
-        gather_words(slot_codes[1][:, 1, :], 1, G, E)
+        w_rest = late.tile([P, E * A, N], U8, name="w_rest", offset=AT_W_REST, align_bytes=64)
+        ws_rest = late.tile([P, E * A, HALF + GAP], U8, name="ws_rest", offset=AT_WS_REST, align_bytes=64)
+        w_t = [w_first, w_rest]
+        ws_t = [ws_first, ws_rest]
+        load_scales(ws_rest, 1)
         last_two = E - 2
-        gather_words(slot_codes[2][:, 1, 0 : 2 * C], 2, G, last_two)
-        gather_words(slot_codes[2][:, 1, 2 * C : 3 * C], 2, last_two, E - 1)
-        gather_words(slot_codes[2][:, 1, 3 * C : G * C], 2, E - 1, E)
+        for e0, e1 in ((0, G), (G, last_two), (last_two, E)):
+            load_words(w_rest[:, A * e0 : A * e1, :], 1, e0, e1)
+        gather_words(2, 0, G)
+        gather_words(1, 2, E, MIDDLE)
+        gather_words(2, G, last_two)
+        gather_words(2, last_two, E - 1)
+        gather_words(2, E - 1, E)
 
         wp_raw = keep.tile([P, 4, M], F32, name="wp_raw", tag="codes", align_bytes=64)
         nc.sync.dma_start(out=wp_raw[:], in_=wp.rearrange("(p j) f -> p j f", j=4))
@@ -152,9 +175,9 @@ def tile_moe_nxt_lin_relu_kernel(tc, xT, w_words, w_scales, b, wp, gate, offs, p
         def multiply(sums, e, r, a):
             nc.tensor.matmul_mx(
                 out=sums,
-                lhsT=w_t[r // 2][e // G][:, e % G * A + a, 2 * P * (r % 2) : 2 * P * (r % 2 + 1)].bitcast(FP4X4),
-                lhsT_scale=ws_t[:, e * A + a, P * r : P * (r + 1)],
-                rhs=slot_codes[a][:, e // G, e % G * C : (e % G + 1) * C].bitcast(FP8X4),
+                lhsT=w_t[r // 2][:, e * A + a, 2 * P * (r % 2) : 2 * P * (r % 2 + 1)].bitcast(FP4X4),
+                lhsT_scale=ws_t[r // 2][:, e * A + a, P * (r % 2) : P * (r % 2 + 1)],
+                rhs=slot_words(a, e, e + 1).bitcast(FP8X4),
                 rhs_scale=slot_planes[a][:, e * C : (e + 1) * C],
                 start=(a == 0),
                 stop=(a == A - 1),
@@ -175,20 +198,22 @@ def tile_moe_nxt_lin_relu_kernel(tc, xT, w_words, w_scales, b, wp, gate, offs, p
             for e in range(e0, e1):
                 activate(acc[:, e - e0, :], e, r)
 
-        for e0 in (0, G):
-            open_sums = [bank(e0 + i, C) for i in range(G)]
-            for a in range(A):
-                for i in range(G):
-                    multiply(open_sums[i][:], e0 + i, 0, a)
-            for i in range(G):
-                activate(open_sums[i][:], e0 + i, 0, on_vector=(e0 + i == E - 1))
+        open_sums = [bank(e, C) for e in range(E)]
+        for e in range(E):
+            multiply(open_sums[e][:], e, 0, 0)
+        for e in range(E):
+            for a in range(1, A):
+                multiply(open_sums[e][:], e, 0, a)
+            activate(open_sums[e][:], e, 0, on_vector=(e >= last_two))
         sum_by_sum(4, 0, G, 1)
         sum_by_sum(5, G, last_two, 1)
         sum_by_sum(6, last_two, E, 1)
         sum_by_sum(7, 0, G, 2)
         sum_by_sum(0, G, last_two, 2)
-        sum_by_sum(1, last_two, E, 2)
-        sum_by_sum(2, 0, G, 3)
+        sum_by_sum(1, 0, 2, 3)
+        sum_by_sum(2, last_two, E - 1, 2)
+        sum_by_sum(3, E - 1, E, 2)
+        sum_by_sum(2, 2, G, 3)
         sum_by_sum(3, G, last_two, 3)
         sum_by_sum(4, last_two, E, 3)
 
@@ -198,15 +223,16 @@ def tile_moe_nxt_lin_relu_kernel(tc, xT, w_words, w_scales, b, wp, gate, offs, p
 
         gated = [[keep.tile([P, T], F32, name=f"gated0_{k}") for k in range(2)]]
         gated = gated + [[late.tile([P, T], F32, name=f"gated1_{k}", offset=AT_GATED + k * T * 4, align_bytes=64) for k in range(2)]]
-        early_half = [[keep.tile([P, 2 * P], F32, name=f"early{r}_{k}") for k in range(2)] for r in range(2, R)]
-        late_half = [[late.tile([P, 2 * P], F32, name=f"late{r}_{k}", offset=AT_LATE + (2 * k + r - 2) * 2 * P * 4, align_bytes=64) for k in range(2)] for r in range(2, R)]
+        last = T - P
+        gated_early = [[keep.tile([P, last], F32, name=f"early{r}_{k}") for k in range(2)] for r in range(2, R)]
+        gated_last = [[late.tile([P, P], F32, name=f"late{r}_{k}", offset=AT_LAST + (2 * k + r - 2) * P * 4, align_bytes=64) for k in range(2)] for r in range(2, R)]
 
         def product(r, k, t0, t1):
             if r < 2:
                 return gated[r][k][:, t0:t1]
-            if t0 < 2 * P:
-                return early_half[r - 2][k][:, t0:t1]
-            return late_half[r - 2][k][:, t0 - 2 * P : t1 - 2 * P]
+            if t0 < last:
+                return gated_early[r - 2][k][:, t0:t1]
+            return gated_last[r - 2][k][:]
 
         c_rows = keep.tile([P, B * N], BF16, name="c_rows")
 
@@ -230,12 +256,14 @@ def tile_moe_nxt_lin_relu_kernel(tc, xT, w_words, w_scales, b, wp, gate, offs, p
             round_rows(0, B, r, r + 1, turned[:].rearrange("t b n -> t (b n)"))
 
         wp_codes = keep.tile([P, M], U32, name="wp_codes", align_bytes=64)
-        wp_planes = late.tile([P, M], U8, name="wp_planes", offset=AT_LATE + 4 * 2 * P * 4, align_bytes=64)
+        wp_planes = late.tile([P, M], U8, name="wp_planes", offset=AT_LAST + 4 * P * 4, align_bytes=64)
 
         c_b = [keep.tile([P, 4 * P], BF16, name=f"c_b{t}", align_bytes=64) for t in range(B)]
         for t in range(B):
-            if t % 2 == 0:
-                fetch(2, t * P, (t + 2) * P)
+            if t == 0:
+                fetch(2, 0, last)
+            if t == B - 1:
+                fetch(2, last, T)
             fetch(3, t * P, (t + 1) * P)
             turned = bank(t % 2, 2, P)
             for r in range(2, R):
@@ -245,7 +273,11 @@ def tile_moe_nxt_lin_relu_kernel(tc, xT, w_words, w_scales, b, wp, gate, offs, p
             pairs = c_rows[:, t * N : (t + 1) * N].bitcast(F32)
             for u in range(2):
                 nc.tensor.transpose(back[:, u, :], pairs[:, u * P : (u + 1) * P], ident[:])
-            nc.scalar.copy(out=c_b[t][:].bitcast(F32).rearrange("p (t u) -> p t u", u=2), in_=back[:].rearrange("p u t -> p t u"))
+            dst = c_b[t][:].bitcast(F32).rearrange("p (t u) -> p t u", u=2)
+            if t < B - 2:
+                nc.scalar.copy(out=dst, in_=back[:].rearrange("p u t -> p t u"))
+            else:
+                nc.vector.tensor_copy(out=dst, in_=back[:].rearrange("p u t -> p t u"))
 
         for f0, f1 in ((0, 2 * P), (2 * P, M)):
             nc.vector.quantize_mx(

@@ -18,13 +18,17 @@ NARROW = 704
 VECTOR_SHARE = (352, 0, 128)
 LIVE_RUNS = ((0, 4), (32, 96), (96, 100))
 GAP = 64
-WS_BYTES = E * A * (HALF + GAP)
 LAP = 64
-AT_PLANES = (2 * E - 2) * C * 4 - LAP
-AT_WS_REST = AT_PLANES + WIDE
-AT_W_REST = AT_WS_REST + WS_BYTES
-AT_X_FIRST = AT_W_REST + E * A * N
-AT_LAST = AT_X_FIRST + 4 * T * 4
+X_BYTES = 4 * T * 4
+W_BYTES = E * A * N
+AT_W_REST = (2 * E - 2) * C * 4
+AT_PLANES = AT_W_REST + W_BYTES - LAP
+AT_X2 = AT_PLANES + WIDE
+AT_WS_REST = AT_X2 - LAP
+AT_X0 = AT_X2 + X_BYTES
+AT_W_FIRST = AT_X0 + X_BYTES - LAP
+AT_SHIFTED = AT_W_FIRST + W_BYTES
+AT_LAST = AT_SHIFTED + 4 * T * 2
 AT_GATED = AT_LAST + P * 4 - LAP
 FLOPS = 2 * K * N * E * C + 2 * N * M * T
 BYTES = 4 * K * T + E * K * N // 2 + E * K * N // 32 + 4 * N * E + 4 * N * M + 4 * 2 * T + 2 * 128 * 128 + 4 * M * T
@@ -53,14 +57,12 @@ def tile_moe_nxt_lin_relu_kernel(tc, xT, w_words, w_scales, b, wp, gate, offs, p
 
         offs_t = keep.tile([P, S // 16], U16, name="offs_t")
         pos_t = [keep.tile([P, T // 16], U16, name=f"pos_t{k}") for k in range(2)]
-        x_raw = [late.tile([P, 4, T], F32, name="x_raw0", offset=AT_X_FIRST, align_bytes=64)]
-        x_raw = x_raw + [keep.tile([P, 4, T], F32, name=f"x_raw{a}") for a in range(1, A)]
-        w_first = keep.tile([P, E * A, N], U8, name="w_first", align_bytes=64)
-        ws_first = keep.tile([P, E * A, HALF + GAP], U8, name="ws_first", align_bytes=64)
-        b_t = keep.tile([P, R, E], F32, name="b_t")
+        x_raw = [
+            late.tile([P, 4, T], F32, name="x_raw0", offset=AT_X0, align_bytes=64),
+            keep.tile([P, 4, T], F32, name="x_raw1"),
+            late.tile([P, 4, T], F32, name="x_raw2", offset=AT_X2, align_bytes=64),
+        ]
         gate_in = keep.tile([P, 2, 8], F32, name="gate_in")
-
-        nc.vector.memset(ws_first[:, :, 0:HALF].bitcast(I32), 0)
 
         for a in range(A):
             nc.sync.dma_start(out=x_raw[a][:], in_=xT[512 * a : 512 * (a + 1), :].rearrange("(p j) t -> p j t", j=4))
@@ -69,12 +71,11 @@ def tile_moe_nxt_lin_relu_kernel(tc, xT, w_words, w_scales, b, wp, gate, offs, p
         nc.sync.dma_start(out=gate_in[:, :, 0:4], in_=gate[:, 0, :].rearrange("k (p i) -> p k i", i=4))
         nc.sync.dma_start(pos_t[0][:], pos1)
         nc.sync.dma_start(pos_t[1][:], pos2)
-        nc.sync.dma_start(out=b_t[:], in_=b.rearrange("(r p) e -> p r e", p=P))
 
         word_rows = w_words.rearrange("e a p c -> p (e a) c")
 
         def load_words(dst, h, e0, e1):
-            nc.sync.dma_start(out=dst.bitcast(I32), in_=word_rows[:, A * e0 : A * e1, N * h : N * (h + 1)].bitcast(I32))
+            nc.sync.dma_start(out=dst[:, A * e0 : A * e1, :].bitcast(I32), in_=word_rows[:, A * e0 : A * e1, N * h : N * (h + 1)].bitcast(I32))
 
         scale_rows = w_scales.rearrange("e a q n -> q (e a) n")
 
@@ -82,9 +83,6 @@ def tile_moe_nxt_lin_relu_kernel(tc, xT, w_words, w_scales, b, wp, gate, offs, p
             for i in range(4):
                 nc.sync.dma_start(out=dst[i:P:32, :, 0:HALF].bitcast(I32), in_=scale_rows[i:16:4, :, HALF * h : HALF * (h + 1)].bitcast(I32))
 
-        load_scales(ws_first, 0)
-        for g in range(2):
-            load_words(w_first[:, G * A * g : G * A * (g + 1), :], 0, G * g, G * (g + 1))
 
         ident = keep.tile([P, P], F32, name="ident")
         make_identity(nc, ident[:])
@@ -92,10 +90,14 @@ def tile_moe_nxt_lin_relu_kernel(tc, xT, w_words, w_scales, b, wp, gate, offs, p
         codes = keep.tile([P, (A - 1) * T + NARROW], I32, name="codes", tag="codes", align_bytes=64)
         nc.vector.memset(codes[:, A * T :], 0)
         first = [(A - 1 - a) * T for a in range(A)]
-        planes = late.tile([P, WIDE + WS_BYTES + LAP], U8, name="planes", offset=AT_PLANES, align_bytes=64)
+        planes = late.tile([P, WIDE], U8, name="planes", offset=AT_PLANES, align_bytes=64)
         packed = keep.tile([P, S], U8, name="packed", align_bytes=64)
         nc.vector.memset(planes[:].bitcast(I32), 0)
-        x_b = [keep.tile([P, T, 4], BF16, name=f"x_b{a}", align_bytes=64) for a in range(A)]
+        x_b = [
+            late.tile([P, T, 4], BF16, name="x_b0", offset=AT_SHIFTED, align_bytes=64),
+            keep.tile([P, T, 4], BF16, name="x_b1", align_bytes=64),
+            late.tile([P, T, 4], BF16, name="x_b2", offset=0, align_bytes=64),
+        ]
 
         def interleaved(dst, src):
             return dst.rearrange("p (c i) j -> p c j i", i=4), src.rearrange("p j (c i) -> p c j i", i=4)
@@ -129,9 +131,15 @@ def tile_moe_nxt_lin_relu_kernel(tc, xT, w_words, w_scales, b, wp, gate, offs, p
         def gather_words(a, e0, e1, width=NARROW):
             gather(slot_words(a, e0, e1), codes[:, first[a] : first[a] + width].bitcast(U32), e0, e1)
 
+        last_two = E - 2
         interleave_pass(0)
         quantise_pass(0)
-        shifted = late.tile([P, A - 1, S], U8, name="shifted", offset=AT_X_FIRST, align_bytes=64)
+        ws_first = late.tile([P, E * A, HALF + GAP], U8, name="ws_first", offset=AT_X0, align_bytes=64)
+        load_scales(ws_first, 0)
+        w_first = late.tile([P, E * A, N], U8, name="w_first", offset=AT_W_FIRST, align_bytes=64)
+        for g in range(2):
+            load_words(w_first, 0, G * g, G * (g + 1))
+        shifted = late.tile([P, A - 1, S], U8, name="shifted", offset=AT_SHIFTED, align_bytes=64)
         nc.vector.memset(shifted[:].bitcast(I32), 0)
         slot_planes = [packed[:], shifted[:, 0, :], shifted[:, 1, :]]
         for g in range(2):
@@ -146,16 +154,18 @@ def tile_moe_nxt_lin_relu_kernel(tc, xT, w_words, w_scales, b, wp, gate, offs, p
             for lo, hi in LIVE_RUNS:
                 nc.sync.dma_start(out=slot_planes[a][lo:hi, :].bitcast(I32), in_=packed[4 * a + lo : 4 * a + hi, :].bitcast(I32))
 
+        b_t = late.tile([P, R, E], F32, name="b_t", offset=AT_PLANES + T, align_bytes=64)
+        nc.sync.dma_start(out=b_t[:], in_=b.rearrange("(r p) e -> p r e", p=P))
         w_rest = late.tile([P, E * A, N], U8, name="w_rest", offset=AT_W_REST, align_bytes=64)
-        ws_rest = late.tile([P, E * A, HALF + GAP], U8, name="ws_rest", offset=AT_WS_REST, align_bytes=64)
         w_t = [w_first, w_rest]
+        ws_rest = late.tile([P, E * A, HALF + GAP], U8, name="ws_rest", offset=AT_WS_REST, align_bytes=64)
         ws_t = [ws_first, ws_rest]
         load_scales(ws_rest, 1)
-        last_two = E - 2
         for e0, e1 in ((0, G), (G, last_two), (last_two, E)):
-            load_words(w_rest[:, A * e0 : A * e1, :], 1, e0, e1)
+            load_words(w_rest, 1, e0, e1)
+        gather_words(1, 2, 3)
         gather_words(2, 0, G)
-        gather_words(1, 2, E, MIDDLE)
+        gather_words(1, 3, E, MIDDLE)
         gather_words(2, G, last_two)
         gather_words(2, last_two, E - 1)
         gather_words(2, E - 1, E)
@@ -172,15 +182,15 @@ def tile_moe_nxt_lin_relu_kernel(tc, xT, w_words, w_scales, b, wp, gate, offs, p
 
         y = [keep.tile([P, S], F32, name=f"y{r}") for r in range(R)]
 
-        def multiply(sums, e, r, a):
+        def multiply(sums, e, r, a, start, stop):
             nc.tensor.matmul_mx(
                 out=sums,
                 lhsT=w_t[r // 2][:, e * A + a, 2 * P * (r % 2) : 2 * P * (r % 2 + 1)].bitcast(FP4X4),
                 lhsT_scale=ws_t[r // 2][:, e * A + a, P * (r % 2) : P * (r % 2 + 1)],
                 rhs=slot_words(a, e, e + 1).bitcast(FP8X4),
                 rhs_scale=slot_planes[a][:, e * C : (e + 1) * C],
-                start=(a == 0),
-                stop=(a == A - 1),
+                start=start,
+                stop=stop,
             )
 
         def activate(sums, e, r, on_vector=False):
@@ -194,20 +204,26 @@ def tile_moe_nxt_lin_relu_kernel(tc, xT, w_words, w_scales, b, wp, gate, offs, p
             acc = bank(at, e1 - e0, C)
             for e in range(e0, e1):
                 for a in range(A):
-                    multiply(acc[:, e - e0, :], e, r, a)
+                    multiply(acc[:, e - e0, :], e, r, a, a == 0, a == A - 1)
             for e in range(e0, e1):
                 activate(acc[:, e - e0, :], e, r)
 
-        open_sums = [bank(e, C) for e in range(E)]
-        for e in range(E):
-            multiply(open_sums[e][:], e, 0, 0)
-        for e in range(E):
-            for a in range(1, A):
-                multiply(open_sums[e][:], e, 0, a)
-            activate(open_sums[e][:], e, 0, on_vector=(e >= last_two))
-        sum_by_sum(4, 0, G, 1)
-        sum_by_sum(5, G, last_two, 1)
-        sum_by_sum(6, last_two, E, 1)
+        early = [(0, 0, G), (0, G, last_two), (0, last_two, E - 1), (0, E - 1, E), (1, 0, G), (1, G, last_two), (1, last_two, E)]
+        open_sums = [bank(i, e1 - e0, C) for i, (r, e0, e1) in enumerate(early)]
+
+        def run_passes(i, a0, a1):
+            r, e0, e1 = early[i]
+            for a in range(a0, a1):
+                for e in range(e0, e1):
+                    multiply(open_sums[i][:, e - e0, :], e, r, a, a == 0 and e == e0, a == A - 1 and e == e1 - 1)
+            if a1 == A:
+                for e in range(e0, e1):
+                    activate(open_sums[i][:, e - e0, :], e, r, on_vector=(r == 0 and e >= last_two))
+
+        for i in range(len(early)):
+            run_passes(i, 0, 1)
+        for i in range(len(early)):
+            run_passes(i, 1, A)
         sum_by_sum(7, 0, G, 2)
         sum_by_sum(0, G, last_two, 2)
         sum_by_sum(1, 0, 2, 3)

@@ -15,7 +15,7 @@ BANKS = 8
 WIDE = 1408
 MIDDLE = 1024
 NARROW = 704
-VECTOR_SHARE = (352, 0, 128)
+VECTOR_SHARE = (352, 64, 128)
 LIVE_RUNS = ((0, 4), (32, 96), (96, 100))
 GAP = 64
 LAP = 64
@@ -87,7 +87,7 @@ def tile_moe_nxt_lin_relu_kernel(tc, xT, w_words, w_scales, b, wp, gate, offs, p
         ident = keep.tile([P, P], F32, name="ident")
         make_identity(nc, ident[:])
 
-        codes = keep.tile([P, (A - 1) * T + NARROW], I32, name="codes", tag="codes", align_bytes=64)
+        codes = keep.tile([P, (A - 1) * T + WIDE], I32, name="codes", tag="codes", align_bytes=64)
         nc.vector.memset(codes[:, A * T :], 0)
         first = [(A - 1 - a) * T for a in range(A)]
         planes = late.tile([P, WIDE], U8, name="planes", offset=AT_PLANES, align_bytes=64)
@@ -117,7 +117,7 @@ def tile_moe_nxt_lin_relu_kernel(tc, xT, w_words, w_scales, b, wp, gate, offs, p
                 in_=x_b[a][:].rearrange("p c j -> p (c j)"),
             )
 
-        ahead = S + 2 * C
+        ahead = S + 3 * C
         slot_first = keep.tile([P, ahead], U32, name="slot_first", align_bytes=64)
         slot_rest = late.tile([P, A * S - ahead], U32, name="slot_rest", offset=0, align_bytes=64)
 
@@ -140,14 +140,12 @@ def tile_moe_nxt_lin_relu_kernel(tc, xT, w_words, w_scales, b, wp, gate, offs, p
         for g in range(2):
             load_words(w_first, 0, G * g, G * (g + 1))
         shifted = late.tile([P, A - 1, S], U8, name="shifted", offset=AT_SHIFTED, align_bytes=64)
-        nc.vector.memset(shifted[:].bitcast(I32), 0)
         slot_planes = [packed[:], shifted[:, 0, :], shifted[:, 1, :]]
-        for g in range(2):
-            gather_words(0, G * g, G * (g + 1))
+        gather_words(0, 0, E, WIDE)
         interleave_pass(1)
         quantise_pass(1)
         interleave_pass(2)
-        gather_words(1, 0, 2)
+        gather_words(1, 0, 3)
         quantise_pass(2)
         gather(packed[:], planes[:, 0:WIDE], 0, E)
         for a in range(1, A):
@@ -161,11 +159,10 @@ def tile_moe_nxt_lin_relu_kernel(tc, xT, w_words, w_scales, b, wp, gate, offs, p
         ws_rest = late.tile([P, E * A, HALF + GAP], U8, name="ws_rest", offset=AT_WS_REST, align_bytes=64)
         ws_t = [ws_first, ws_rest]
         load_scales(ws_rest, 1)
-        for e0, e1 in ((0, G), (G, last_two), (last_two, E)):
-            load_words(w_rest, 1, e0, e1)
-        gather_words(1, 2, 3)
-        gather_words(2, 0, G)
+        for e0 in range(0, E, 2):
+            load_words(w_rest, 1, e0, e0 + 2)
         gather_words(1, 3, E, MIDDLE)
+        gather_words(2, 0, G)
         gather_words(2, G, last_two)
         gather_words(2, last_two, E - 1)
         gather_words(2, E - 1, E)
@@ -208,7 +205,24 @@ def tile_moe_nxt_lin_relu_kernel(tc, xT, w_words, w_scales, b, wp, gate, offs, p
             for e in range(e0, e1):
                 activate(acc[:, e - e0, :], e, r)
 
-        early = [(0, 0, G), (0, G, last_two), (0, last_two, E - 1), (0, E - 1, E), (1, 0, G), (1, G, last_two), (1, last_two, E)]
+        early = [(0, 0, G), (0, G, last_two), (0, last_two, E - 1), (0, E - 1, E), (1, 0, G)]
+        def warm_up(at, passes):
+            idle = bank(at, HALF)
+            for g in range(passes):
+                warm_pass(idle, g)
+
+        def warm_pass(idle, g):
+            nc.tensor.matmul_mx(
+                out=idle[:],
+                lhsT=w_first[:, g, 0 : 2 * P].bitcast(FP4X4),
+                lhsT_scale=ws_first[:, g, 0:P],
+                rhs=slot_first[:, ahead - HALF : ahead].bitcast(FP8X4),
+                rhs_scale=ws_first[:, g, 0:HALF],
+                start=True,
+                stop=True,
+            )
+
+        warm_up(0, 4)
         open_sums = [bank(i, e1 - e0, C) for i, (r, e0, e1) in enumerate(early)]
 
         def run_passes(i, a0, a1):
@@ -224,12 +238,16 @@ def tile_moe_nxt_lin_relu_kernel(tc, xT, w_words, w_scales, b, wp, gate, offs, p
             run_passes(i, 0, 1)
         for i in range(len(early)):
             run_passes(i, 1, A)
-        sum_by_sum(7, 0, G, 2)
-        sum_by_sum(0, G, last_two, 2)
+        sum_by_sum(2, G, last_two, 1)
+        sum_by_sum(3, last_two, E, 1)
+        warm_up(2, 1)
+        sum_by_sum(7, 0, 2, 2)
         sum_by_sum(1, 0, 2, 3)
+        sum_by_sum(0, 2, G, 2)
+        sum_by_sum(5, 2, G, 3)
+        sum_by_sum(6, G, last_two, 2)
         sum_by_sum(2, last_two, E - 1, 2)
         sum_by_sum(3, E - 1, E, 2)
-        sum_by_sum(2, 2, G, 3)
         sum_by_sum(3, G, last_two, 3)
         sum_by_sum(4, last_two, E, 3)
 
@@ -280,7 +298,8 @@ def tile_moe_nxt_lin_relu_kernel(tc, xT, w_words, w_scales, b, wp, gate, offs, p
                 fetch(2, 0, last)
             if t == B - 1:
                 fetch(2, last, T)
-            fetch(3, t * P, (t + 1) * P)
+            if t != 1:
+                fetch(3, t * P, (t + (2 if t == 0 else 1)) * P)
             turned = bank(t % 2, 2, P)
             for r in range(2, R):
                 turn(turned[:, r - 2, :], r, t)

@@ -206,23 +206,6 @@ def tile_moe_nxt_lin_relu_kernel(tc, xT, w_words, w_scales, b, wp, gate, offs, p
                 activate(acc[:, e - e0, :], e, r)
 
         early = [(0, 0, G), (0, G, last_two), (0, last_two, E - 1), (0, E - 1, E), (1, 0, G)]
-        def warm_up(at, passes):
-            idle = bank(at, HALF)
-            for g in range(passes):
-                warm_pass(idle, g)
-
-        def warm_pass(idle, g):
-            nc.tensor.matmul_mx(
-                out=idle[:],
-                lhsT=w_first[:, g, 0 : 2 * P].bitcast(FP4X4),
-                lhsT_scale=ws_first[:, g, 0:P],
-                rhs=slot_first[:, ahead - HALF : ahead].bitcast(FP8X4),
-                rhs_scale=ws_first[:, g, 0:HALF],
-                start=True,
-                stop=True,
-            )
-
-        warm_up(0, 4)
         open_sums = [bank(i, e1 - e0, C) for i, (r, e0, e1) in enumerate(early)]
 
         def run_passes(i, a0, a1):
@@ -240,7 +223,6 @@ def tile_moe_nxt_lin_relu_kernel(tc, xT, w_words, w_scales, b, wp, gate, offs, p
             run_passes(i, 1, A)
         sum_by_sum(2, G, last_two, 1)
         sum_by_sum(3, last_two, E, 1)
-        warm_up(2, 1)
         sum_by_sum(7, 0, 2, 2)
         sum_by_sum(1, 0, 2, 3)
         sum_by_sum(0, 2, G, 2)

@@ -231,7 +231,8 @@ def tile_moe_nxt_lin_relu_kernel(tc, xT, w_words, w_scales, b, wp, gate, offs, p
         sum_by_sum(2, last_two, E - 1, 2)
         sum_by_sum(3, E - 1, E, 2)
         sum_by_sum(3, G, last_two, 3)
-        sum_by_sum(4, last_two, E, 3)
+        sum_by_sum(4, last_two, E - 1, 3)
+        sum_by_sum(5, E - 1, E, 3)
 
         wp_b = late.tile([P, M, 4], BF16, name="wp_b", offset=0, align_bytes=64)
         dst, src = interleaved(wp_b[:], wp_raw[:])
@@ -270,6 +271,18 @@ def tile_moe_nxt_lin_relu_kernel(tc, xT, w_words, w_scales, b, wp, gate, offs, p
             for t in range(B):
                 turn(turned[:, t, :], r, t)
             round_rows(0, B, r, r + 1, turned[:].rearrange("t b n -> t (b n)"))
+
+        idle = bank(5, HALF)
+        for g in range(5):
+            nc.tensor.matmul_mx(
+                out=idle[:],
+                lhsT=w_first[:, g, 0 : 2 * P].bitcast(FP4X4),
+                lhsT_scale=ws_first[:, g, 0:P],
+                rhs=slot_first[:, 0:HALF].bitcast(FP8X4),
+                rhs_scale=packed[:, 0:HALF],
+                start=True,
+                stop=True,
+            )
 
         wp_codes = keep.tile([P, M], U32, name="wp_codes", align_bytes=64)
         wp_planes = late.tile([P, M], U8, name="wp_planes", offset=AT_LAST + 4 * P * 4, align_bytes=64)

@@ -288,49 +288,64 @@ def tile_moe_nxt_lin_relu_kernel(tc, xT, w_words, w_scales, b, wp, gate, offs, p
         wp_planes = late.tile([P, M], U8, name="wp_planes", offset=AT_LAST + 4 * P * 4, align_bytes=64)
 
         c_b = [keep.tile([P, 4 * P], BF16, name=f"c_b{t}", align_bytes=64) for t in range(B)]
-        for t in range(B):
-            if t == 0:
-                fetch(2, 0, last)
-            if t == B - 1:
-                fetch(2, last, T)
-            if t != 1:
-                fetch(3, t * P, (t + (2 if t == 0 else 1)) * P)
+        c_codes = [keep.tile([P, P], U32, name=f"c_codes{t}", align_bytes=64) for t in range(B)]
+        c_planes = [keep.tile([P, P], U8, name=f"c_planes{t}", align_bytes=64) for t in range(B)]
+        result = [keep.tile([P, M // P, P + GAP // 4], F32, name=f"result{t}") for t in range(B)]
+        out_rows = out.rearrange("(f p) t -> p f t", p=P)
+
+        def turn_block(t):
             turned = bank(t % 2, 2, P)
             for r in range(2, R):
                 turn(turned[:, r - 2, :], r, t)
             round_rows(t, t + 1, 2, R, turned[:].rearrange("t r n -> t (r n)"))
-            back = bank(2 + t % 2, 2, P)
+
+        def turn_back(t):
+            back = bank((2, 3, 6, 7)[t], 2, P)
             pairs = c_rows[:, t * N : (t + 1) * N].bitcast(F32)
             for u in range(2):
                 nc.tensor.transpose(back[:, u, :], pairs[:, u * P : (u + 1) * P], ident[:])
             dst = c_b[t][:].bitcast(F32).rearrange("p (t u) -> p t u", u=2)
-            if t < B - 2:
+            if t < 2:
                 nc.scalar.copy(out=dst, in_=back[:].rearrange("p u t -> p t u"))
             else:
                 nc.vector.tensor_copy(out=dst, in_=back[:].rearrange("p u t -> p t u"))
 
+        def quantise_block(t):
+            nc.vector.quantize_mx(out=c_codes[t][:].bitcast(FP8X4), scales=c_planes[t][:], in_=c_b[t][:])
+
+        def project(t):
+            cut = 3 if t < 2 else 2
+            sums = [bank(4 + t, M // P, P)] * 2 if t < 2 else [bank(2 * t - 4, 2, P), bank(2 * t - 3, 1, P)]
+            for f in range(M // P):
+                nc.tensor.matmul_mx(
+                    out=sums[0][:, f, :] if f < cut else sums[1][:, 0, :],
+                    lhsT=wp_codes[:, f * P : (f + 1) * P].bitcast(FP8X4),
+                    lhsT_scale=wp_planes[:, f * P : (f + 1) * P],
+                    rhs=c_codes[t][:].bitcast(FP8X4),
+                    rhs_scale=c_planes[t][:],
+                    start=True,
+                    stop=True,
+                )
+            nc.scalar.copy(out=result[t][:, 0:cut, 0:P], in_=sums[0][:])
+            if cut < 3:
+                nc.vector.tensor_copy(out=result[t][:, cut:3, 0:P], in_=sums[1][:])
+            nc.sync.dma_start(out=out_rows[:, :, t * P : (t + 1) * P], in_=result[t][:, :, 0:P])
+
+        fetch(2, 0, last)
+        fetch(3, 0, 2 * P)
+        fetch(3, 2 * P, last)
+        for r in range(2, R):
+            fetch(r, last, T)
         for f0, f1 in ((0, 2 * P), (2 * P, M)):
             nc.vector.quantize_mx(
                 out=wp_codes[:, f0:f1].bitcast(FP8X4), scales=wp_planes[:, f0:f1], in_=wp_b[:, f0:f1, :].rearrange("p c j -> p (c j)")
             )
-
-        out_rows = out.rearrange("(f p) t -> p f t", p=P)
+        for t in range(B + 2):
+            if 2 <= t:
+                quantise_block(t - 2)
+            if t < B:
+                turn_block(t)
+            if 1 <= t <= B:
+                turn_back(t - 1)
         for t in range(B):
-            c_codes = keep.tile([P, P], U32, name=f"c_codes{t}", align_bytes=64)
-            c_planes = keep.tile([P, P], U8, name=f"c_planes{t}", align_bytes=64)
-            nc.vector.quantize_mx(out=c_codes[:].bitcast(FP8X4), scales=c_planes[:], in_=c_b[t][:])
-            sums = [bank(4 + 2 * (t % 2), 2, P), bank(5 + 2 * (t % 2), 1, P)]
-            for f in range(M // P):
-                nc.tensor.matmul_mx(
-                    out=sums[f // 2][:, f % 2, :],
-                    lhsT=wp_codes[:, f * P : (f + 1) * P].bitcast(FP8X4),
-                    lhsT_scale=wp_planes[:, f * P : (f + 1) * P],
-                    rhs=c_codes[:].bitcast(FP8X4),
-                    rhs_scale=c_planes[:],
-                    start=True,
-                    stop=True,
-                )
-            result = keep.tile([P, M // P, P + GAP // 4], F32, name=f"result{t}")
-            nc.scalar.copy(out=result[:, 0:2, 0:P], in_=sums[0][:])
-            nc.vector.tensor_copy(out=result[:, 2:3, 0:P], in_=sums[1][:])
-            nc.sync.dma_start(out=out_rows[:, :, t * P : (t + 1) * P], in_=result[:, :, 0:P])
+            project(t)

@@ -17,6 +17,7 @@ MIDDLE = 1024
 NARROW = 704
 VECTOR_SHARE = (352, 64, 128)
 LIVE_RUNS = ((0, 4), (32, 96), (96, 100))
+WARM_UPS = 5
 GAP = 64
 LAP = 64
 X_BYTES = 4 * T * 4
@@ -205,6 +206,19 @@ def tile_moe_nxt_lin_relu_kernel(tc, xT, w_words, w_scales, b, wp, gate, offs, p
             for e in range(e0, e1):
                 activate(acc[:, e - e0, :], e, r)
 
+        def warm_up(at, passes):
+            idle = bank(at, HALF)
+            for g in range(passes):
+                nc.tensor.matmul_mx(
+                    out=idle[:],
+                    lhsT=w_first[:, g, 0 : 2 * P].bitcast(FP4X4),
+                    lhsT_scale=ws_first[:, g, 0:P],
+                    rhs=slot_first[:, 0:HALF].bitcast(FP8X4),
+                    rhs_scale=packed[:, 0:HALF],
+                    start=True,
+                    stop=True,
+                )
+
         early = [(0, 0, G), (0, G, last_two), (0, last_two, E - 1), (0, E - 1, E), (1, 0, G)]
         open_sums = [bank(i, e1 - e0, C) for i, (r, e0, e1) in enumerate(early)]
 
@@ -223,6 +237,7 @@ def tile_moe_nxt_lin_relu_kernel(tc, xT, w_words, w_scales, b, wp, gate, offs, p
             run_passes(i, 1, A)
         sum_by_sum(2, G, last_two, 1)
         sum_by_sum(3, last_two, E, 1)
+        warm_up(2, 1)
         sum_by_sum(7, 0, 2, 2)
         sum_by_sum(1, 0, 2, 3)
         sum_by_sum(0, 2, G, 2)
@@ -272,17 +287,7 @@ def tile_moe_nxt_lin_relu_kernel(tc, xT, w_words, w_scales, b, wp, gate, offs, p
                 turn(turned[:, t, :], r, t)
             round_rows(0, B, r, r + 1, turned[:].rearrange("t b n -> t (b n)"))
 
-        idle = bank(5, HALF)
-        for g in range(5):
-            nc.tensor.matmul_mx(
-                out=idle[:],
-                lhsT=w_first[:, g, 0 : 2 * P].bitcast(FP4X4),
-                lhsT_scale=ws_first[:, g, 0:P],
-                rhs=slot_first[:, 0:HALF].bitcast(FP8X4),
-                rhs_scale=packed[:, 0:HALF],
-                start=True,
-                stop=True,
-            )
+        warm_up(5, WARM_UPS - 1)
 
         wp_codes = keep.tile([P, M], U32, name="wp_codes", align_bytes=64)
         wp_planes = late.tile([P, M], U8, name="wp_planes", offset=AT_LAST + 4 * P * 4, align_bytes=64)

@@ -299,13 +299,13 @@ def tile_moe_nxt_lin_relu_kernel(tc, xT, w_words, w_scales, b, wp, gate, offs, p
         out_rows = out.rearrange("(f p) t -> p f t", p=P)
 
         def turn_block(t):
-            turned = bank(t % 2, 2, P)
+            turned = bank(t % 3, 2, P)
             for r in range(2, R):
                 turn(turned[:, r - 2, :], r, t)
             round_rows(t, t + 1, 2, R, turned[:].rearrange("t r n -> t (r n)"))
 
         def turn_back(t):
-            back = bank((2, 3, 6, 7)[t], 2, P)
+            back = bank((6, 7, 3, 4)[t], 2, P)
             pairs = c_rows[:, t * N : (t + 1) * N].bitcast(F32)
             for u in range(2):
                 nc.tensor.transpose(back[:, u, :], pairs[:, u * P : (u + 1) * P], ident[:])
@@ -320,7 +320,7 @@ def tile_moe_nxt_lin_relu_kernel(tc, xT, w_words, w_scales, b, wp, gate, offs, p
 
         def project(t):
             cut = 3 if t < 2 else 2
-            sums = [bank(4 + t, M // P, P)] * 2 if t < 2 else [bank(2 * t - 4, 2, P), bank(2 * t - 3, 1, P)]
+            sums = [bank((5, 1)[t], M // P, P)] * 2 if t < 2 else [bank((2, 0)[t - 2], 2, P), bank(4 + t, 1, P)]
             for f in range(M // P):
                 nc.tensor.matmul_mx(
                     out=sums[0][:, f, :] if f < cut else sums[1][:, 0, :],

@@ -80,9 +80,12 @@ def tile_moe_nxt_lin_relu_kernel(tc, xT, w_words, w_scales, b, wp, gate, offs, p
 
         scale_rows = w_scales.rearrange("e a q n -> q (e a) n")
 
-        def load_scales(dst, h):
-            for i in range(4):
-                nc.sync.dma_start(out=dst[i:P:32, :, 0:HALF].bitcast(I32), in_=scale_rows[i:16:4, :, HALF * h : HALF * (h + 1)].bitcast(I32))
+        def load_scales(dst, h, parts=1):
+            rows = E * A // parts
+            for lo in range(0, E * A, rows):
+                for i in range(4):
+                    src = scale_rows[i:16:4, lo : lo + rows, HALF * h : HALF * (h + 1)]
+                    nc.sync.dma_start(out=dst[i:P:32, lo : lo + rows, 0:HALF].bitcast(I32), in_=src.bitcast(I32))
 
 
         ident = keep.tile([P, P], F32, name="ident")
@@ -154,12 +157,13 @@ def tile_moe_nxt_lin_relu_kernel(tc, xT, w_words, w_scales, b, wp, gate, offs, p
                 nc.sync.dma_start(out=slot_planes[a][lo:hi, :].bitcast(I32), in_=packed[4 * a + lo : 4 * a + hi, :].bitcast(I32))
 
         b_t = late.tile([P, R, E], F32, name="b_t", offset=AT_PLANES + T, align_bytes=64)
-        nc.sync.dma_start(out=b_t[:], in_=b.rearrange("(r p) e -> p r e", p=P))
+        for h in range(2):
+            nc.sync.dma_start(out=b_t[:, 2 * h : 2 * h + 2, :], in_=b.rearrange("(r p) e -> p r e", p=P)[:, 2 * h : 2 * h + 2, :])
         w_rest = late.tile([P, E * A, N], U8, name="w_rest", offset=AT_W_REST, align_bytes=64)
         w_t = [w_first, w_rest]
         ws_rest = late.tile([P, E * A, HALF + GAP], U8, name="ws_rest", offset=AT_WS_REST, align_bytes=64)
         ws_t = [ws_first, ws_rest]
-        load_scales(ws_rest, 1)
+        load_scales(ws_rest, 1, parts=2)
         for e0 in range(0, E, 2):
             load_words(w_rest, 1, e0, e0 + 2)
         gather_words(1, 3, E, MIDDLE)

from contextlib import ExitStack

import concourse.mybir as mybir
from concourse.masks import make_identity

K, T, E, C, N, M = 1536, 512, 8, 128, 512, 384
P = 128
A = K // 512
R = N // P
B = T // P
S = E * C
G = E // 2
HALF = N // 2
BANKS = 8
WIDE = 1408
MIDDLE = 1024
NARROW = 704
VECTOR_SHARE = (352, 64, 128)
LIVE_RUNS = ((0, 4), (32, 96), (96, 100))
WARM_UPS = 5
GAP = 64
LAP = 64
X_BYTES = 4 * T * 4
W_BYTES = E * A * N
AT_W_REST = (2 * E - 2) * C * 4
AT_PLANES = AT_W_REST + W_BYTES - LAP
AT_X2 = AT_PLANES + WIDE
AT_WS_REST = AT_X2 - LAP
AT_X0 = AT_X2 + X_BYTES
AT_W_FIRST = AT_X0 + X_BYTES - LAP
AT_SHIFTED = AT_W_FIRST + W_BYTES
AT_LAST = AT_SHIFTED + 4 * T * 2
AT_GATED = AT_LAST + P * 4 - LAP
FLOPS = 2 * K * N * E * C + 2 * N * M * T
BYTES = 4 * K * T + E * K * N // 2 + E * K * N // 32 + 4 * N * E + 4 * N * M + 4 * 2 * T + 2 * 128 * 128 + 4 * M * T

F32 = mybir.dt.float32
BF16 = mybir.dt.bfloat16
I32 = mybir.dt.int32
U32 = mybir.dt.uint32
U16 = mybir.dt.uint16
U8 = mybir.dt.uint8
FP8X4 = mybir.dt.float8_e4m3fn_x4
FP4X4 = mybir.dt.float4_e2m1fn_x4
ACT = mybir.ActivationFunctionType
ALU = mybir.AluOpType


def tile_moe_nxt_lin_relu_kernel(tc, xT, w_words, w_scales, b, wp, gate, offs, pos1, pos2, out):
    nc = tc.nc
    with ExitStack() as ctx:
        keep = ctx.enter_context(tc.tile_pool(name="keep", bufs=1))
        late = ctx.enter_context(tc.tile_pool(name="late", bufs=1))
        psum = ctx.enter_context(tc.psum_pool(name="psum", bufs=1))

        def bank(i, *shape):
            return psum.tile([P, *shape], F32, name=f"bank{i}", tag=f"bank{i}")

        offs_t = keep.tile([P, S // 16], U16, name="offs_t")
        pos_t = [keep.tile([P, T // 16], U16, name=f"pos_t{k}") for k in range(2)]
        x_raw = [
            late.tile([P, 4, T], F32, name="x_raw0", offset=AT_X0, align_bytes=64),
            keep.tile([P, 4, T], F32, name="x_raw1"),
            late.tile([P, 4, T], F32, name="x_raw2", offset=AT_X2, align_bytes=64),
        ]
        gate_in = keep.tile([P, 2, 8], F32, name="gate_in")

        for a in range(A):
            nc.sync.dma_start(out=x_raw[a][:], in_=xT[512 * a : 512 * (a + 1), :].rearrange("(p j) t -> p j t", j=4))
            if a == 0:
                nc.sync.dma_start(offs_t[:], offs)
        nc.sync.dma_start(out=gate_in[:, :, 0:4], in_=gate[:, 0, :].rearrange("k (p i) -> p k i", i=4))
        nc.sync.dma_start(pos_t[0][:], pos1)
        nc.sync.dma_start(pos_t[1][:], pos2)

        word_rows = w_words.rearrange("e a p c -> p (e a) c")

        def load_words(dst, h, e0, e1):
            nc.sync.dma_start(out=dst[:, A * e0 : A * e1, :].bitcast(I32), in_=word_rows[:, A * e0 : A * e1, N * h : N * (h + 1)].bitcast(I32))

        scale_rows = w_scales.rearrange("e a q n -> q (e a) n")

        def load_scales(dst, h, parts=1):
            rows = E * A // parts
            for lo in range(0, E * A, rows):
                for i in range(4):
                    src = scale_rows[i:16:4, lo : lo + rows, HALF * h : HALF * (h + 1)]
                    nc.sync.dma_start(out=dst[i:P:32, lo : lo + rows, 0:HALF].bitcast(I32), in_=src.bitcast(I32))


        ident = keep.tile([P, P], F32, name="ident")
        make_identity(nc, ident[:])

        codes = keep.tile([P, (A - 1) * T + WIDE], I32, name="codes", tag="codes", align_bytes=64)
        nc.vector.memset(codes[:, A * T :], 0)
        first = [(A - 1 - a) * T for a in range(A)]
        planes = late.tile([P, WIDE], U8, name="planes", offset=AT_PLANES, align_bytes=64)
        packed = keep.tile([P, S], U8, name="packed", align_bytes=64)
        nc.vector.memset(planes[:].bitcast(I32), 0)
        x_b = [
            late.tile([P, T, 4], BF16, name="x_b0", offset=AT_SHIFTED, align_bytes=64),
            keep.tile([P, T, 4], BF16, name="x_b1", align_bytes=64),
            late.tile([P, T, 4], BF16, name="x_b2", offset=0, align_bytes=64),
        ]

        def interleaved(dst, src):
            return dst.rearrange("p (c i) j -> p c j i", i=4), src.rearrange("p j (c i) -> p c j i", i=4)

        def interleave_pass(a):
            cut = T - VECTOR_SHARE[a]
            dst, src = interleaved(x_b[a][:, 0:cut, :], x_raw[a][:, :, 0:cut])
            nc.scalar.activation(out=dst, in_=src, func=ACT.Copy)
            if cut < T:
                dst, src = interleaved(x_b[a][:, cut:T, :], x_raw[a][:, :, cut:T])
                nc.vector.tensor_copy(out=dst, in_=src)

        def quantise_pass(a):
            nc.vector.quantize_mx(
                out=codes[:, first[a] : first[a] + T].bitcast(FP8X4),
                scales=planes[4 * a : P, 0:T],
                in_=x_b[a][:].rearrange("p c j -> p (c j)"),
            )

        ahead = S + 3 * C
        slot_first = keep.tile([P, ahead], U32, name="slot_first", align_bytes=64)
        slot_rest = late.tile([P, A * S - ahead], U32, name="slot_rest", offset=0, align_bytes=64)

        def slot_words(a, e0, e1):
            lo, hi = a * S + e0 * C, a * S + e1 * C
            return slot_first[:, lo:hi] if lo < ahead else slot_rest[:, lo - ahead : hi - ahead]

        def gather(dst, window, e0, e1):
            nc.vector.tensor_copy(out=dst, in_=window.indirect(offs_t[:, e0 * C // 16 : e1 * C // 16]))

        def gather_words(a, e0, e1, width=NARROW):
            gather(slot_words(a, e0, e1), codes[:, first[a] : first[a] + width].bitcast(U32), e0, e1)

        last_two = E - 2
        interleave_pass(0)
        quantise_pass(0)
        ws_first = late.tile([P, E * A, HALF + GAP], U8, name="ws_first", offset=AT_X0, align_bytes=64)
        load_scales(ws_first, 0)
        w_first = late.tile([P, E * A, N], U8, name="w_first", offset=AT_W_FIRST, align_bytes=64)
        for g in range(2):
            load_words(w_first, 0, G * g, G * (g + 1))
        shifted = late.tile([P, A - 1, S], U8, name="shifted", offset=AT_SHIFTED, align_bytes=64)
        slot_planes = [packed[:], shifted[:, 0, :], shifted[:, 1, :]]
        gather_words(0, 0, E, WIDE)
        interleave_pass(1)
        quantise_pass(1)
        interleave_pass(2)
        gather_words(1, 0, 3)
        quantise_pass(2)
        gather(packed[:], planes[:, 0:WIDE], 0, E)
        for a in range(1, A):
            for lo, hi in LIVE_RUNS:
                nc.sync.dma_start(out=slot_planes[a][lo:hi, :].bitcast(I32), in_=packed[4 * a + lo : 4 * a + hi, :].bitcast(I32))

        b_t = late.tile([P, R, E], F32, name="b_t", offset=AT_PLANES + T, align_bytes=64)
        for h in range(2):
            nc.sync.dma_start(out=b_t[:, 2 * h : 2 * h + 2, :], in_=b.rearrange("(r p) e -> p r e", p=P)[:, 2 * h : 2 * h + 2, :])
        w_rest = late.tile([P, E * A, N], U8, name="w_rest", offset=AT_W_REST, align_bytes=64)
        w_t = [w_first, w_rest]
        ws_rest = late.tile([P, E * A, HALF + GAP], U8, name="ws_rest", offset=AT_WS_REST, align_bytes=64)
        ws_t = [ws_first, ws_rest]
        load_scales(ws_rest, 1, parts=2)
        for e0 in range(0, E, 2):
            load_words(w_rest, 1, e0, e0 + 2)
        gather_words(1, 3, E, MIDDLE)
        gather_words(2, 0, G)
        gather_words(2, G, last_two)
        gather_words(2, last_two, E - 1)
        gather_words(2, E - 1, E)

        wp_raw = keep.tile([P, 4, M], F32, name="wp_raw", tag="codes", align_bytes=64)
        nc.sync.dma_start(out=wp_raw[:], in_=wp.rearrange("(p j) f -> p j f", j=4))

        gate_t = keep.tile([P, 2, T], F32, name="gate_t")
        for k in range(2):
            spread = bank(BANKS - 2 + k, 4, P)
            for i in range(4):
                nc.tensor.transpose(spread[:, i, :], gate_in[:, k, i : i + 1].to_broadcast([P, P]), ident[:])
            nc.scalar.copy(out=gate_t[:, k, :].rearrange("m (p i) -> m p i", i=4), in_=spread[:].rearrange("m i p -> m p i"))

        y = [keep.tile([P, S], F32, name=f"y{r}") for r in range(R)]

        def multiply(sums, e, r, a, start, stop):
            nc.tensor.matmul_mx(
                out=sums,
                lhsT=w_t[r // 2][:, e * A + a, 2 * P * (r % 2) : 2 * P * (r % 2 + 1)].bitcast(FP4X4),
                lhsT_scale=ws_t[r // 2][:, e * A + a, P * (r % 2) : P * (r % 2 + 1)],
                rhs=slot_words(a, e, e + 1).bitcast(FP8X4),
                rhs_scale=slot_planes[a][:, e * C : (e + 1) * C],
                start=start,
                stop=stop,
            )

        def activate(sums, e, r, on_vector=False):
            dst = y[r][:, e * C : (e + 1) * C]
            if on_vector:
                nc.vector.tensor_scalar(dst, sums, b_t[:, r, e : e + 1], 0.0, ALU.add, ALU.max)
            else:
                nc.scalar.activation(out=dst, in_=sums, func=ACT.Relu, bias=b_t[:, r, e : e + 1])

        def sum_by_sum(at, e0, e1, r):
            acc = bank(at, e1 - e0, C)
            for e in range(e0, e1):
                for a in range(A):
                    multiply(acc[:, e - e0, :], e, r, a, a == 0, a == A - 1)
            for e in range(e0, e1):
                activate(acc[:, e - e0, :], e, r)

        def warm_up(at, passes):
            idle = bank(at, HALF)
            for g in range(passes):
                nc.tensor.matmul_mx(
                    out=idle[:],
                    lhsT=w_first[:, g, 0 : 2 * P].bitcast(FP4X4),
                    lhsT_scale=ws_first[:, g, 0:P],
                    rhs=slot_first[:, 0:HALF].bitcast(FP8X4),
                    rhs_scale=packed[:, 0:HALF],
                    start=True,
                    stop=True,
                )

        early = [(0, 0, G), (0, G, last_two), (0, last_two, E - 1), (0, E - 1, E), (1, 0, G)]
        open_sums = [bank(i, e1 - e0, C) for i, (r, e0, e1) in enumerate(early)]

        def run_passes(i, a0, a1):
            r, e0, e1 = early[i]
            for a in range(a0, a1):
                for e in range(e0, e1):
                    multiply(open_sums[i][:, e - e0, :], e, r, a, a == 0 and e == e0, a == A - 1 and e == e1 - 1)
            if a1 == A:
                for e in range(e0, e1):
                    activate(open_sums[i][:, e - e0, :], e, r, on_vector=(r == 0 and e >= last_two))

        for i in range(len(early)):
            run_passes(i, 0, 1)
        for i in range(len(early)):
            run_passes(i, 1, A)
        sum_by_sum(2, G, last_two, 1)
        sum_by_sum(3, last_two, E, 1)
        warm_up(2, 1)
        sum_by_sum(7, 0, 2, 2)
        sum_by_sum(1, 0, 2, 3)
        sum_by_sum(0, 2, G, 2)
        sum_by_sum(5, 2, G, 3)
        sum_by_sum(6, G, last_two, 2)
        sum_by_sum(2, last_two, E - 1, 2)
        sum_by_sum(3, E - 1, E, 2)
        sum_by_sum(3, G, last_two, 3)
        sum_by_sum(4, last_two, E - 1, 3)
        sum_by_sum(5, E - 1, E, 3)

        wp_b = late.tile([P, M, 4], BF16, name="wp_b", offset=0, align_bytes=64)
        dst, src = interleaved(wp_b[:], wp_raw[:])
        nc.scalar.activation(out=dst, in_=src, func=ACT.Copy)

        gated = [[keep.tile([P, T], F32, name=f"gated0_{k}") for k in range(2)]]
        gated = gated + [[late.tile([P, T], F32, name=f"gated1_{k}", offset=AT_GATED + k * T * 4, align_bytes=64) for k in range(2)]]
        last = T - P
        gated_early = [[keep.tile([P, last], F32, name=f"early{r}_{k}") for k in range(2)] for r in range(2, R)]
        gated_last = [[late.tile([P, P], F32, name=f"late{r}_{k}", offset=AT_LAST + (2 * k + r - 2) * P * 4, align_bytes=64) for k in range(2)] for r in range(2, R)]

        def product(r, k, t0, t1):
            if r < 2:
                return gated[r][k][:, t0:t1]
            if t0 < last:
                return gated_early[r - 2][k][:, t0:t1]
            return gated_last[r - 2][k][:]

        c_rows = keep.tile([P, B * N], BF16, name="c_rows")

        def fetch(r, t0, t1):
            for k in range(2):
                nc.vector.tensor_tensor(product(r, k, t0, t1), y[r][:].indirect(pos_t[k][:, t0 // 16 : t1 // 16]), gate_t[:, k, t0:t1], ALU.mult)

        def turn(dst, r, t):
            for k in range(2):
                nc.tensor.matmul(dst, lhsT=product(r, k, t * P, (t + 1) * P), rhs=ident[:], is_transpose=True, start=(k == 0), stop=(k == 1))

        def round_rows(t0, t1, r0, r1, sums):
            dst = c_rows[:, t0 * N : t1 * N].rearrange("t (b u p e) -> t b u p e", u=2, p=P, e=2)[:, :, :, 32 * r0 : 32 * r1, :]
            nc.scalar.copy(out=dst, in_=sums.rearrange("t (b p u e) -> t b u p e", p=32 * (r1 - r0), u=2, e=2))

        for r in range(2):
            fetch(r, 0, T)
            turned = bank(3 + r, B, P)
            for t in range(B):
                turn(turned[:, t, :], r, t)
            round_rows(0, B, r, r + 1, turned[:].rearrange("t b n -> t (b n)"))

        warm_up(5, WARM_UPS - 1)

        wp_codes = keep.tile([P, M], U32, name="wp_codes", align_bytes=64)
        wp_planes = late.tile([P, M], U8, name="wp_planes", offset=AT_LAST + 4 * P * 4, align_bytes=64)

        c_b = [keep.tile([P, 4 * P], BF16, name=f"c_b{t}", align_bytes=64) for t in range(B)]
        c_codes = [keep.tile([P, P], U32, name=f"c_codes{t}", align_bytes=64) for t in range(B)]
        c_planes = [keep.tile([P, P], U8, name=f"c_planes{t}", align_bytes=64) for t in range(B)]
        result = [keep.tile([P, M // P, P + GAP // 4], F32, name=f"result{t}") for t in range(B)]
        out_rows = out.rearrange("(f p) t -> p f t", p=P)

        def turn_block(t):
            turned = bank(t % 3, 2, P)
            for r in range(2, R):
                turn(turned[:, r - 2, :], r, t)
            round_rows(t, t + 1, 2, R, turned[:].rearrange("t r n -> t (r n)"))

        def turn_back(t):
            back = bank((6, 7, 3, 4)[t], 2, P)
            pairs = c_rows[:, t * N : (t + 1) * N].bitcast(F32)
            for u in range(2):
                nc.tensor.transpose(back[:, u, :], pairs[:, u * P : (u + 1) * P], ident[:])
            dst = c_b[t][:].bitcast(F32).rearrange("p (t u) -> p t u", u=2)
            if t < 2:
                nc.scalar.copy(out=dst, in_=back[:].rearrange("p u t -> p t u"))
            else:
                nc.vector.tensor_copy(out=dst, in_=back[:].rearrange("p u t -> p t u"))

        def quantise_block(t):
            nc.vector.quantize_mx(out=c_codes[t][:].bitcast(FP8X4), scales=c_planes[t][:], in_=c_b[t][:])

        def project(t):
            cut = 3 if t < 2 else 2
            sums = [bank((5, 1)[t], M // P, P)] * 2 if t < 2 else [bank((2, 0)[t - 2], 2, P), bank(4 + t, 1, P)]
            for f in range(M // P):
                nc.tensor.matmul_mx(
                    out=sums[0][:, f, :] if f < cut else sums[1][:, 0, :],
                    lhsT=wp_codes[:, f * P : (f + 1) * P].bitcast(FP8X4),
                    lhsT_scale=wp_planes[:, f * P : (f + 1) * P],
                    rhs=c_codes[t][:].bitcast(FP8X4),
                    rhs_scale=c_planes[t][:],
                    start=True,
                    stop=True,
                )
            nc.scalar.copy(out=result[t][:, 0:cut, 0:P], in_=sums[0][:])
            if cut < 3:
                nc.vector.tensor_copy(out=result[t][:, cut:3, 0:P], in_=sums[1][:])
            nc.sync.dma_start(out=out_rows[:, :, t * P : (t + 1) * P], in_=result[t][:, :, 0:P])

        fetch(2, 0, last)
        fetch(3, 0, 2 * P)
        fetch(3, 2 * P, last)
        for r in range(2, R):
            fetch(r, last, T)
        for f0, f1 in ((0, 2 * P), (2 * P, M)):
            nc.vector.quantize_mx(
                out=wp_codes[:, f0:f1].bitcast(FP8X4), scales=wp_planes[:, f0:f1], in_=wp_b[:, f0:f1, :].rearrange("p c j -> p (c j)")
            )
        for t in range(B + 2):
            if 2 <= t:
                quantise_block(t - 2)
            if t < B:
                turn_block(t)
            if 1 <= t <= B:
                turn_back(t - 1)
        for t in range(B):
            project(t)
